import numpy as np
import ml_dtypes


def mxq(x, axis, fmt="e4m3"):
    dtype, down = {"e4m3": (ml_dtypes.float8_e4m3fn, 7), "e5m2": (ml_dtypes.float8_e5m2, 14)}[fmt]
    v = np.moveaxis(np.asarray(x, np.float32).astype(ml_dtypes.bfloat16).astype(np.float64), axis, -1)
    blocks = v.reshape(v.shape[:-1] + (-1, 32))
    amax = np.abs(blocks).max(-1, keepdims=True)
    byte = np.maximum(np.where(amax > 0, np.frexp(amax)[1] - 1 + 127, 0) - down, 1)
    scale = np.exp2(byte - 127.0)
    codes = (blocks / scale).astype(np.float32).astype(dtype).astype(np.float64)
    return np.moveaxis((codes * scale).reshape(v.shape), -1, axis)


WIDE = False


def mx_kscale(k):
    if not WIDE:
        return np.ones(k)
    levels = np.array([10, -10, 5, -5, 0])
    if k % 512:
        return np.exp2(np.random.permutation(np.resize(levels, k // 32))).repeat(32)
    a = np.empty((k // 512, 16))
    for p in range(k // 512):
        a[p, :8] = np.random.permutation(np.resize(levels, 8))
        for g in range(8):
            far = levels[np.abs(levels - a[p, g]) >= 10]
            a[p, g + 8] = far[np.random.randint(len(far))]
    return np.exp2(a.ravel()).repeat(32)


def f64(x):
    return np.asarray(x).astype(np.float64)


def striped(idx):
    return np.tile(idx.reshape(-1, 16).T, (8, 1)).astype(np.uint16)


def unstriped(offs):
    return offs[:16].T.reshape(-1).astype(np.int64)


E2M1 = np.array([0.0, 0.5, 1.0, 1.5, 2.0, 3.0, 4.0, 6.0, -0.0, -0.5, -1.0, -1.5, -2.0, -3.0, -4.0, -6.0])


def pack_weight(w, fmt):
    k, n = w.shape
    w = f64(np.asarray(w, np.float32).astype(ml_dtypes.bfloat16)).reshape(k // 32, 32, n)
    amax = np.abs(w).max(1)
    if fmt == "e4m3":
        byte = np.frexp(amax)[1] - 1 + 127 - 7
    else:
        mant, ex = np.frexp(amax / 6.0)
        byte = np.where(mant > 0.5, ex, ex - 1) + 127
    byte = np.clip(np.where(amax > 0, byte, 1), 1, 254)
    scaled = (w * np.exp2(127.0 - byte)[:, None, :]).reshape(k, n).astype(np.float32)
    by_word = np.ascontiguousarray(scaled.reshape(k // 512, 128, 4, n).transpose(0, 1, 3, 2))
    if fmt == "e4m3":
        words = by_word.astype(ml_dtypes.float8_e4m3fn).view(np.uint8)
    else:
        c = by_word.astype(ml_dtypes.float4_e2m1fn).view(np.uint8) & 0xF
        words = (c[..., 0::2] | (c[..., 1::2] << 4)).reshape(k // 512, 128, 2 * n)
    return np.ascontiguousarray(words), np.ascontiguousarray(byte.astype(np.uint8).reshape(k // 512, 16, n))


def unpack_weight(words, scales, fmt):
    g, _, n = scales.shape
    words = np.ascontiguousarray(words).reshape(g, 128, n, -1)
    if fmt == "e4m3":
        vals = words.view(ml_dtypes.float8_e4m3fn).astype(np.float64)
    else:
        nib = np.empty((g, 128, n, 4), np.uint8)
        nib[..., 0::2] = words & 0xF
        nib[..., 1::2] = words >> 4
        vals = E2M1[nib]
    vals = vals * np.repeat(np.exp2(scales.astype(np.float64) - 127.0), 8, axis=1)[..., None]
    return vals.transpose(0, 1, 3, 2).reshape(g * 512, n)


def d_relu(v):
    return (v > 0).astype(np.float64)


K, T, E, C, H, N = 128, 512, 2, 256, 1024, 1024


def by_expert(wq, xq):
    return np.concatenate([wq[e].T @ xq[:, e * C:(e + 1) * C] for e in range(E)], axis=1)


def setup_inputs():
    n = np.random.standard_normal
    s = mx_kscale(N)[:, None]
    u = mx_kscale(H)
    dy = pack_weight(n((N, T)) * s, "e4m3")
    w2 = [pack_weight(m, "e2m1") for m in n((E, N, H)) / np.sqrt(N) / s[None] * u[None, None, :]]
    w1 = [pack_weight(m, "e2m1") for m in n((E, H, K)) / np.sqrt(H) / u[None, :, None]]
    return {
        "dy_words": dy[0],
        "dy_scales": dy[1],
        "a": n((H, E * C)).astype(np.float32),
        "w2_words": np.stack([m[0] for m in w2]),
        "w2_scales": np.stack([m[1] for m in w2]),
        "w1_words": np.stack([m[0] for m in w1]),
        "w1_scales": np.stack([m[1] for m in w1]),
        "gate": np.tile(np.random.uniform(0.2, 1.0, E * C), (H, 1)).astype(np.float32),
        "offs": striped(np.random.permutation(T)[:E * C]),
    }


def reference(dy_words, dy_scales, a, w2_words, w2_scales, w1_words, w1_scales, gate, offs):
    idx = unstriped(offs)
    w2 = np.stack([unpack_weight(w2_words[e], w2_scales[e], "e2m1") for e in range(E)])
    w1 = np.stack([unpack_weight(w1_words[e], w1_scales[e], "e2m1") for e in range(E)])
    gq = unpack_weight(dy_words, dy_scales, "e4m3")[:, idx]
    dh = f64(gate) * by_expert(w2, gq)
    da = dh * d_relu(f64(a))
    dx = by_expert(w1, mxq(da, 0, "e4m3"))
    out = np.zeros((K, T))
    out[:, idx] = dx
    return out

@@ -1,0 +1,213 @@
+from contextlib import ExitStack
+
+import concourse.mybir as mybir
+from concourse.masks import make_identity
+
+K, T, E, C, H, N = 128, 512, 2, 256, 1024, 1024
+FLOPS = 2 * E * C * (N * H + H * K)
+BYTES = N * T + N * T // 32 + 4 * H * E * C + E * (N * H + H * K) * 17 // 32 + 4 * E * C + 2 * 128 * 32 + 4 * K * T
+
+F32 = mybir.dt.float32
+BF16 = mybir.dt.bfloat16
+I32 = mybir.dt.int32
+U32 = mybir.dt.uint32
+U16 = mybir.dt.uint16
+U8 = mybir.dt.uint8
+FP8X4 = mybir.dt.float8_e4m3fn_x4
+FP4X4 = mybir.dt.float4_e2m1fn_x4
+ALU = mybir.AluOpType
+ACT = mybir.ActivationFunctionType
+
+P = 128
+PASS = 512
+PASSES = 2
+TILES = E * C // P
+TILES_PER_EXPERT = C // P
+LIST_COLS = P // 16
+
+
+def load_scale_rows(queue, plane, rows):
+    by_row = rows.bitcast(I32).rearrange("g (q r) w -> r q g w", r=4)
+    for r in range(4):
+        queue.dma_start(out=plane[r:P:32, :, :].bitcast(I32), in_=by_row[r])
+
+
+def tile_moe_bdx_mlp_relu_kernel(
+    tc, dy_words, dy_scales, a, w2_words, w2_scales, w1_words, w1_scales, gate, offs, out
+):
+    nc = tc.nc
+    with ExitStack() as ctx:
+        keep = ctx.enter_context(tc.tile_pool(name="keep", bufs=1))
+        psum = ctx.enter_context(tc.psum_pool(name="psum", bufs=2))
+
+        def sb(name, shape, dtype):
+            return keep.tile(shape, dtype, name=name, align_bytes=64)
+
+        offsets = sb("offsets", [P, E * C // 16], U16)
+        dy_win = [sb("dy_win%d" % o, [P, T], I32) for o in range(PASSES)]
+        dy_plane = sb("dy_plane", [P, PASSES, T], U8)
+        w2_plane = sb("w2_plane", [P, E * PASSES, H], U8)
+        w1_plane = sb("w1_plane", [P, E * PASSES, K], U8)
+        w2_sb = [sb("w2_sb%d" % e, [P, PASSES, 2 * H], U8) for e in range(E)]
+        w1_sb = sb("w1_sb", [P, E * PASSES, 2 * K], U8)
+        gate_col = sb("gate_col", [P, TILES], F32)
+        a_sb = [[sb("a_sb%d%d" % (e, s), [P, 4, C], F32) for s in range(PASSES)] for e in range(E)]
+        ident = sb("ident", [P, P], F32)
+        result = sb("result", [P, T], F32)
+
+        for plane in (dy_plane, w2_plane, w1_plane):
+            nc.vector.memset(plane[:].bitcast(I32), 0)
+        make_identity(nc, ident[:])
+
+        def load_dy(o):
+            nc.sync.dma_start(out=dy_win[o][:], in_=dy_words[o].rearrange("p t d -> p (t d)").bitcast(I32))
+
+        def load_w2(e):
+            nc.sync.dma_start(out=w2_sb[e][:].bitcast(I32), in_=w2_words[e].bitcast(I32).rearrange("s p w -> p s w"))
+
+        def load_a(e, s):
+            rows = a[s * PASS : (s + 1) * PASS, e * C : (e + 1) * C]
+            nc.sync.dma_start(out=a_sb[e][s][:], in_=rows.rearrange("(p t) c -> p t c", t=4))
+
+        nc.sync.dma_start(offsets[:], offs)
+        load_dy(0)
+        load_scale_rows(nc.sync, dy_plane, dy_scales)
+        load_dy(1)
+        load_w2(0)
+        load_scale_rows(nc.sync, w2_plane, w2_scales.rearrange("e s f w -> (e s) f w"))
+        with nc.allow_non_contiguous_dma(reason="one gate value a slot, one slot a partition"):
+            nc.sync.dma_start(out=gate_col[:], in_=gate[0].rearrange("(j p) -> p j", p=P))
+        load_a(0, 0)
+        load_a(0, 1)
+        load_w2(1)
+        load_a(1, 0)
+        load_a(1, 1)
+        nc.sync.dma_start(out=w1_sb[:].bitcast(I32), in_=w1_words.bitcast(I32).rearrange("e s p w -> p (e s) w"))
+        load_scale_rows(nc.sync, w1_plane, w1_scales.rearrange("e s f w -> (e s) f w"))
+
+        g_words = [sb("g_words%d" % e, [P, PASSES, C], U32) for e in range(E)]
+        g_scales = [sb("g_scales%d" % e, [P, PASSES, C], U8) for e in range(E)]
+        gated = [[sb("gated%d%d" % (j, h), [P, PASS], BF16) for h in range(PASSES)] for j in range(TILES)]
+        mask = [sb("mask%d" % e, [P, PASSES, C, 4], BF16) for e in range(E)]
+        da = [sb("da%d" % j, [P, PASSES * P * 4], BF16) for j in range(TILES)]
+        da_words = [sb("da_words%d" % j, [P, PASSES, P], U32) for j in range(TILES)]
+        da_scales = [sb("da_scales%d" % j, [P, PASSES, P], U8) for j in range(TILES)]
+        dx = [sb("dx%d" % j, [P, P], F32) for j in range(TILES)]
+        turned = {}
+
+        def slots(j):
+            return offsets[:, j * LIST_COLS : (j + 1) * LIST_COLS]
+
+        def gather(j, count):
+            e, jj = divmod(j, TILES_PER_EXPERT)
+            cols = slice(jj * P, (jj + count) * P)
+            picks = offsets[:, j * LIST_COLS : (j + count) * LIST_COLS]
+            for o in range(PASSES):
+                nc.vector.tensor_copy(g_words[e][:, o, cols], dy_win[o][:].bitcast(U32).indirect(picks))
+                nc.vector.tensor_copy(g_scales[e][:, o, cols], dy_plane[:, o, :].indirect(picks))
+
+        def first_product(j):
+            e, jj = divmod(j, TILES_PER_EXPERT)
+            cols = slice(jj * P, (jj + 1) * P)
+            for h in range(PASSES):
+                sums = psum.tile([P, PASS], F32, name="sums%d" % h)
+                for o in range(PASSES):
+                    nc.tensor.matmul_mx(
+                        out=sums[:],
+                        lhsT=g_words[e][:, o, cols].bitcast(FP8X4),
+                        lhsT_scale=g_scales[e][:, o, cols],
+                        rhs=w2_sb[e][:, o, h * 2 * PASS : (h + 1) * 2 * PASS].bitcast(FP4X4),
+                        rhs_scale=w2_plane[:, e * PASSES + o, h * PASS : (h + 1) * PASS],
+                        start=(o == 0),
+                        stop=(o == PASSES - 1),
+                    )
+                nc.scalar.activation(
+                    out=gated[j][h][:].rearrange("c (u p v) -> c u p v", u=2, v=2),
+                    in_=sums[:].rearrange("c (p u v) -> c u p v", u=2, v=2),
+                    func=ACT.Copy,
+                    scale=gate_col[:, j : j + 1],
+                )
+
+        def turn(j):
+            bank = psum.tile([P, 2, PASSES, P], F32, name="turned")
+            for h in range(PASSES):
+                pairs = gated[j][h][:].bitcast(F32)
+                for u in range(2):
+                    nc.tensor.transpose(bank[:, u, h, :], pairs[:, u * P : (u + 1) * P], ident[:])
+            turned[j] = bank
+
+        def make_mask(e, s):
+            nc.vector.tensor_scalar(
+                mask[e][:, s, :, :].rearrange("p (c i) t -> p c t i", i=4),
+                a_sb[e][s][:].rearrange("p t (c i) -> p c t i", i=4),
+                0.0,
+                None,
+                op0=ALU.is_gt,
+            )
+
+        def apply_mask(j):
+            e, jj = divmod(j, TILES_PER_EXPERT)
+            nc.vector.tensor_tensor(
+                da[j][:].rearrange("p (s c u v) -> p s c u v", s=PASSES, u=2, v=2),
+                turned[j][:].bitcast(BF16).rearrange("p u s (c v) -> p s c u v", v=2),
+                mask[e][:, :, jj * P : (jj + 1) * P, :].rearrange("p s c (u v) -> p s c u v", v=2),
+                ALU.mult,
+            )
+
+        def quantize(j):
+            nc.vector.quantize_mx(
+                out=da_words[j][:].rearrange("p s c -> p (s c)").bitcast(FP8X4),
+                scales=da_scales[j][:].rearrange("p s c -> p (s c)"),
+                in_=da[j][:],
+            )
+
+        def second_product(j):
+            e = j // TILES_PER_EXPERT
+            sums = psum.tile([P, P], F32, name="dx_sums")
+            for s in range(PASSES):
+                nc.tensor.matmul_mx(
+                    out=sums[:],
+                    lhsT=w1_sb[:, e * PASSES + s, :].bitcast(FP4X4),
+                    lhsT_scale=w1_plane[:, e * PASSES + s, :],
+                    rhs=da_words[j][:, s, :].bitcast(FP8X4),
+                    rhs_scale=da_scales[j][:, s, :],
+                    start=(s == 0),
+                    stop=(s == PASSES - 1),
+                )
+            nc.scalar.copy(dx[j][:], sums[:])
+
+        def scatter(j):
+            nc.vector.tensor_copy(result[:].indirect(slots(j)), dx[j][:])
+
+        gather(0, 1)
+        first_product(0)
+        gather(1, 1)
+        first_product(1)
+        turn(0)
+        gather(2, 2)
+        first_product(2)
+        turn(1)
+        first_product(3)
+        make_mask(0, 0)
+        make_mask(0, 1)
+        apply_mask(0)
+        apply_mask(1)
+        turn(2)
+        turn(3)
+        quantize(0)
+        quantize(1)
+        second_product(0)
+        second_product(1)
+        make_mask(1, 0)
+        make_mask(1, 1)
+        apply_mask(2)
+        scatter(0)
+        apply_mask(3)
+        quantize(2)
+        quantize(3)
+        second_product(2)
+        second_product(3)
+        scatter(1)
+        scatter(2)
+        scatter(3)
+        nc.sync.dma_start(out=out, in_=result[:])

@@ -5,7 +5,7 @@ from concourse.masks import make_identity
 
 K, T, E, C, H, N = 128, 512, 2, 256, 1024, 1024
 FLOPS = 2 * E * C * (N * H + H * K)
-BYTES = N * T + N * T // 32 + 4 * H * E * C + E * (N * H + H * K) * 17 // 32 + 4 * E * C + 2 * 128 * 32 + 4 * K * T
+BYTES = N * T * 33 // 32 + E * (N * H + H * K) * 17 // 32 + 4 * H * E * C + 4 * E * C + 2 * 128 * E * C // 16 + 4 * K * T
 
 F32 = mybir.dt.float32
 BF16 = mybir.dt.bfloat16
@@ -19,17 +19,22 @@ ALU = mybir.AluOpType
 ACT = mybir.ActivationFunctionType
 
 P = 128
-PASS = 512
-PASSES = 2
-TILES = E * C // P
+PACK = 4
+PASS = P * PACK
+N_PASSES = N // PASS
+HALVES = H // PASS
 TILES_PER_EXPERT = C // P
-LIST_COLS = P // 16
+TILES = E * TILES_PER_EXPERT
+LIST_ROWS = 16
+RUN = 4
+WORD_GROUPS = ((0,), (1,), (2, 3))
+SUM_BANKS, TURN_BANKS, DX_BANKS = 3, 3, 2
 
 
-def load_scale_rows(queue, plane, rows):
+def load_scale_rows(nc, plane, rows):
     by_row = rows.bitcast(I32).rearrange("g (q r) w -> r q g w", r=4)
     for r in range(4):
-        queue.dma_start(out=plane[r:P:32, :, :].bitcast(I32), in_=by_row[r])
+        nc.sync.dma_start(out=plane[r:P:32, :, :].bitcast(I32), in_=by_row[r])
 
 
 def tile_moe_bdx_mlp_relu_kernel(
@@ -38,176 +43,149 @@ def tile_moe_bdx_mlp_relu_kernel(
     nc = tc.nc
     with ExitStack() as ctx:
         keep = ctx.enter_context(tc.tile_pool(name="keep", bufs=1))
-        psum = ctx.enter_context(tc.psum_pool(name="psum", bufs=2))
+        shared = ctx.enter_context(tc.tile_pool(name="shared", bufs=1))
+        psum = ctx.enter_context(tc.psum_pool(name="psum", bufs=1))
 
         def sb(name, shape, dtype):
             return keep.tile(shape, dtype, name=name, align_bytes=64)
 
-        offsets = sb("offsets", [P, E * C // 16], U16)
-        dy_win = [sb("dy_win%d" % o, [P, T], I32) for o in range(PASSES)]
-        dy_plane = sb("dy_plane", [P, PASSES, T], U8)
-        w2_plane = sb("w2_plane", [P, E * PASSES, H], U8)
-        w1_plane = sb("w1_plane", [P, E * PASSES, K], U8)
-        w2_sb = [sb("w2_sb%d" % e, [P, PASSES, 2 * H], U8) for e in range(E)]
-        w1_sb = sb("w1_sb", [P, E * PASSES, 2 * K], U8)
+        offsets = sb("offsets", [P, E * C // LIST_ROWS], U16)
+        dy_window = sb("dy_window", [P, N_PASSES, T], I32)
+        dy_plane = sb("dy_plane", [P, N_PASSES, T], U8)
+        w2_sb = [sb("w2_sb%d" % e, [P, N_PASSES, 2 * H], U8) for e in range(E)]
+        w2_plane = sb("w2_plane", [P, E * N_PASSES, H], U8)
+        w1_sb = sb("w1_sb", [P, E * HALVES, 2 * K], U8)
+        w1_plane = sb("w1_plane", [P, E * HALVES, K], U8)
+        a_sb = [[sb("a_sb%d%d" % (e, h), [P, PACK, C], F32) for h in range(HALVES)] for e in range(E)]
+        gate_rows = shared.tile([P, P], F32, name="gate_rows", tag="gate_rows_then_last_words", align_bytes=64)
         gate_col = sb("gate_col", [P, TILES], F32)
-        a_sb = [[sb("a_sb%d%d" % (e, s), [P, 4, C], F32) for s in range(PASSES)] for e in range(E)]
         ident = sb("ident", [P, P], F32)
-        result = sb("result", [P, T], F32)
+        warm = sb("warm", [P, 16], F32)
 
-        for plane in (dy_plane, w2_plane, w1_plane):
-            nc.vector.memset(plane[:].bitcast(I32), 0)
+        nc.vector.memset(warm[:, 0:1], 0.0)
+        nc.scalar.copy(warm[:, 8:9], warm[:, 0:1])
+
+        nc.gpsimd.memset(dy_plane[:].bitcast(I32), 0)
+        nc.vector.memset(gate_rows[:], 0.0)
+        nc.vector.memset(w2_plane[:].bitcast(I32), 0)
         make_identity(nc, ident[:])
-
-        def load_dy(o):
-            nc.sync.dma_start(out=dy_win[o][:], in_=dy_words[o].rearrange("p t d -> p (t d)").bitcast(I32))
+        nc.gpsimd.memset(w1_plane[:].bitcast(I32), 0)
 
         def load_w2(e):
             nc.sync.dma_start(out=w2_sb[e][:].bitcast(I32), in_=w2_words[e].bitcast(I32).rearrange("s p w -> p s w"))
 
-        def load_a(e, s):
-            rows = a[s * PASS : (s + 1) * PASS, e * C : (e + 1) * C]
-            nc.sync.dma_start(out=a_sb[e][s][:], in_=rows.rearrange("(p t) c -> p t c", t=4))
+        def load_a(e, h):
+            rows = a[h * PASS : (h + 1) * PASS, e * C : (e + 1) * C]
+            nc.sync.dma_start(out=a_sb[e][h][:], in_=rows.rearrange("(p t) c -> p t c", t=PACK))
 
         nc.sync.dma_start(offsets[:], offs)
-        load_dy(0)
-        load_scale_rows(nc.sync, dy_plane, dy_scales)
-        load_dy(1)
+        nc.sync.dma_start(out=dy_window[:], in_=dy_words.rearrange("o p t d -> p o (t d)").bitcast(I32))
+        load_scale_rows(nc, dy_plane, dy_scales)
         load_w2(0)
-        load_scale_rows(nc.sync, w2_plane, w2_scales.rearrange("e s f w -> (e s) f w"))
-        with nc.allow_non_contiguous_dma(reason="one gate value a slot, one slot a partition"):
-            nc.sync.dma_start(out=gate_col[:], in_=gate[0].rearrange("(j p) -> p j", p=P))
+        nc.sync.dma_start(out=gate_rows[0:TILES, :], in_=gate[0].rearrange("(j p) -> j p", p=P))
+        load_scale_rows(nc, w2_plane, w2_scales.rearrange("e s f w -> (e s) f w"))
         load_a(0, 0)
-        load_a(0, 1)
         load_w2(1)
+        load_a(0, 1)
         load_a(1, 0)
         load_a(1, 1)
+        load_scale_rows(nc, w1_plane, w1_scales.rearrange("e s f w -> (e s) f w"))
         nc.sync.dma_start(out=w1_sb[:].bitcast(I32), in_=w1_words.bitcast(I32).rearrange("e s p w -> p (e s) w"))
-        load_scale_rows(nc.sync, w1_plane, w1_scales.rearrange("e s f w -> (e s) f w"))
 
-        g_words = [sb("g_words%d" % e, [P, PASSES, C], U32) for e in range(E)]
-        g_scales = [sb("g_scales%d" % e, [P, PASSES, C], U8) for e in range(E)]
-        gated = [[sb("gated%d%d" % (j, h), [P, PASS], BF16) for h in range(PASSES)] for j in range(TILES)]
-        mask = [sb("mask%d" % e, [P, PASSES, C, 4], BF16) for e in range(E)]
-        da = [sb("da%d" % j, [P, PASSES * P * 4], BF16) for j in range(TILES)]
-        da_words = [sb("da_words%d" % j, [P, PASSES, P], U32) for j in range(TILES)]
-        da_scales = [sb("da_scales%d" % j, [P, PASSES, P], U8) for j in range(TILES)]
-        dx = [sb("dx%d" % j, [P, P], F32) for j in range(TILES)]
-        turned = {}
+        gate_turned = psum.tile([P, C], F32, name="dx_bank", bufs=DX_BANKS)
+        nc.tensor.transpose(gate_turned[:, 0:P], gate_rows[:], ident[:])
+        nc.scalar.copy(gate_col[:], gate_turned[:, 0:TILES])
 
-        def slots(j):
-            return offsets[:, j * LIST_COLS : (j + 1) * LIST_COLS]
+        def list_of(first_tile, tiles):
+            return offsets[:, first_tile * P // LIST_ROWS : (first_tile + tiles) * P // LIST_ROWS]
 
-        def gather(j, count):
-            e, jj = divmod(j, TILES_PER_EXPERT)
-            cols = slice(jj * P, (jj + count) * P)
-            picks = offsets[:, j * LIST_COLS : (j + count) * LIST_COLS]
-            for o in range(PASSES):
-                nc.vector.tensor_copy(g_words[e][:, o, cols], dy_win[o][:].bitcast(U32).indirect(picks))
-                nc.vector.tensor_copy(g_scales[e][:, o, cols], dy_plane[:, o, :].indirect(picks))
+        g_words = {}
+        for group in WORD_GROUPS:
+            shape = [P, N_PASSES, P * len(group)]
+            if group == WORD_GROUPS[-1]:
+                words = shared.tile(shape, U32, name="g_words_last", tag="gate_rows_then_last_words", align_bytes=64)
+            else:
+                words = sb("g_words%d" % group[0], shape, U32)
+            for o in range(N_PASSES):
+                window = dy_window[:, o, :].bitcast(U32)
+                nc.vector.tensor_copy(words[:, o, :], window.indirect(list_of(group[0], len(group))))
+            for place, j in enumerate(group):
+                g_words[j] = words[:, :, place * P : (place + 1) * P]
+        g_scales = [sb("g_scales%d" % e, [P, N_PASSES, C], U8) for e in range(E)]
+        for e in range(E):
+            for o in range(N_PASSES):
+                picks = list_of(e * TILES_PER_EXPERT, TILES_PER_EXPERT)
+                nc.vector.tensor_copy(g_scales[e][:, o, :], dy_plane[:, o, :].indirect(picks))
 
-        def first_product(j):
-            e, jj = divmod(j, TILES_PER_EXPERT)
-            cols = slice(jj * P, (jj + 1) * P)
-            for h in range(PASSES):
-                sums = psum.tile([P, PASS], F32, name="sums%d" % h)
-                for o in range(PASSES):
-                    nc.tensor.matmul_mx(
-                        out=sums[:],
-                        lhsT=g_words[e][:, o, cols].bitcast(FP8X4),
-                        lhsT_scale=g_scales[e][:, o, cols],
-                        rhs=w2_sb[e][:, o, h * 2 * PASS : (h + 1) * 2 * PASS].bitcast(FP4X4),
-                        rhs_scale=w2_plane[:, e * PASSES + o, h * PASS : (h + 1) * PASS],
-                        start=(o == 0),
-                        stop=(o == PASSES - 1),
-                    )
-                nc.scalar.activation(
-                    out=gated[j][h][:].rearrange("c (u p v) -> c u p v", u=2, v=2),
-                    in_=sums[:].rearrange("c (p u v) -> c u p v", u=2, v=2),
-                    func=ACT.Copy,
-                    scale=gate_col[:, j : j + 1],
+        def first_product(e, h, jj):
+            j = e * TILES_PER_EXPERT + jj
+            sums = psum.tile([P, PASS], F32, name="sum_bank", bufs=SUM_BANKS)
+            for o in range(N_PASSES):
+                nc.tensor.matmul_mx(
+                    out=sums[:],
+                    lhsT=g_words[j][:, o, :].bitcast(FP8X4),
+                    lhsT_scale=g_scales[e][:, o, jj * P : (jj + 1) * P],
+                    rhs=w2_sb[e][:, o, h * 2 * PASS : (h + 1) * 2 * PASS].bitcast(FP4X4),
+                    rhs_scale=w2_plane[:, e * N_PASSES + o, h * PASS : (h + 1) * PASS],
+                    start=(o == 0),
+                    stop=(o == N_PASSES - 1),
                 )
+            gated = sb("gated%d%d" % (j, h), [P, PASS], BF16)
+            nc.scalar.activation(
+                out=gated[:].rearrange("c (u p v) -> c u p v", u=2, v=2),
+                in_=sums[:].rearrange("c (p u v) -> c u p v", u=2, v=2),
+                func=ACT.Copy,
+                scale=gate_col[:, j : j + 1],
+            )
+            return gated
 
-        def turn(j):
-            bank = psum.tile([P, 2, PASSES, P], F32, name="turned")
-            for h in range(PASSES):
-                pairs = gated[j][h][:].bitcast(F32)
+        def quantised_da(e, h):
+            gated = [first_product(e, h, jj) for jj in range(TILES_PER_EXPERT)]
+            turned = psum.tile([P, 2, C], F32, name="turn_bank", bufs=TURN_BANKS)
+            for jj in range(TILES_PER_EXPERT):
+                pairs = gated[jj][:].bitcast(F32)
                 for u in range(2):
-                    nc.tensor.transpose(bank[:, u, h, :], pairs[:, u * P : (u + 1) * P], ident[:])
-            turned[j] = bank
+                    nc.tensor.transpose(turned[:, u, jj * P : (jj + 1) * P], pairs[:, u * P : (u + 1) * P], ident[:])
 
-        def make_mask(e, s):
+            mask = sb("mask%d%d" % (e, h), [P, C, PACK], BF16)
             nc.vector.tensor_scalar(
-                mask[e][:, s, :, :].rearrange("p (c i) t -> p c t i", i=4),
-                a_sb[e][s][:].rearrange("p t (c i) -> p c t i", i=4),
+                mask[:].rearrange("p (c r) t -> p c t r", r=RUN),
+                a_sb[e][h][:].rearrange("p t (c r) -> p c t r", r=RUN),
                 0.0,
                 None,
                 op0=ALU.is_gt,
             )
-
-        def apply_mask(j):
-            e, jj = divmod(j, TILES_PER_EXPERT)
+            da = sb("da%d%d" % (e, h), [P, C * PACK], BF16)
             nc.vector.tensor_tensor(
-                da[j][:].rearrange("p (s c u v) -> p s c u v", s=PASSES, u=2, v=2),
-                turned[j][:].bitcast(BF16).rearrange("p u s (c v) -> p s c u v", v=2),
-                mask[e][:, :, jj * P : (jj + 1) * P, :].rearrange("p s c (u v) -> p s c u v", v=2),
+                da[:].rearrange("p (c u v) -> p c u v", u=2, v=2),
+                turned[:].bitcast(BF16).rearrange("p u (c v) -> p c u v", v=2),
+                mask[:].rearrange("p c (u v) -> p c u v", v=2),
                 ALU.mult,
             )
+            words = sb("da_words%d%d" % (e, h), [P, C], U32)
+            scales = sb("da_scales%d%d" % (e, h), [P, C], U8)
+            nc.vector.quantize_mx(out=words[:].bitcast(FP8X4), scales=scales[:], in_=da[:])
+            return words, scales
 
-        def quantize(j):
-            nc.vector.quantize_mx(
-                out=da_words[j][:].rearrange("p s c -> p (s c)").bitcast(FP8X4),
-                scales=da_scales[j][:].rearrange("p s c -> p (s c)"),
-                in_=da[j][:],
-            )
+        da_mx = [[quantised_da(e, h) for h in range(HALVES)] for e in range(E)]
 
-        def second_product(j):
-            e = j // TILES_PER_EXPERT
-            sums = psum.tile([P, P], F32, name="dx_sums")
-            for s in range(PASSES):
-                nc.tensor.matmul_mx(
-                    out=sums[:],
-                    lhsT=w1_sb[:, e * PASSES + s, :].bitcast(FP4X4),
-                    lhsT_scale=w1_plane[:, e * PASSES + s, :],
-                    rhs=da_words[j][:, s, :].bitcast(FP8X4),
-                    rhs_scale=da_scales[j][:, s, :],
-                    start=(s == 0),
-                    stop=(s == PASSES - 1),
-                )
-            nc.scalar.copy(dx[j][:], sums[:])
-
-        def scatter(j):
-            nc.vector.tensor_copy(result[:].indirect(slots(j)), dx[j][:])
-
-        gather(0, 1)
-        first_product(0)
-        gather(1, 1)
-        first_product(1)
-        turn(0)
-        gather(2, 2)
-        first_product(2)
-        turn(1)
-        first_product(3)
-        make_mask(0, 0)
-        make_mask(0, 1)
-        apply_mask(0)
-        apply_mask(1)
-        turn(2)
-        turn(3)
-        quantize(0)
-        quantize(1)
-        second_product(0)
-        second_product(1)
-        make_mask(1, 0)
-        make_mask(1, 1)
-        apply_mask(2)
-        scatter(0)
-        apply_mask(3)
-        quantize(2)
-        quantize(3)
-        second_product(2)
-        second_product(3)
-        scatter(1)
-        scatter(2)
-        scatter(3)
+        result = sb("result", [P, T], F32)
+        for e in range(E):
+            dx_sums = psum.tile([P, C], F32, name="dx_bank", bufs=DX_BANKS)
+            for jj in range(TILES_PER_EXPERT):
+                cols = slice(jj * P, (jj + 1) * P)
+                for h in range(HALVES):
+                    words, scales = da_mx[e][h]
+                    nc.tensor.matmul_mx(
+                        out=dx_sums[:, cols],
+                        lhsT=w1_sb[:, e * HALVES + h, :].bitcast(FP4X4),
+                        lhsT_scale=w1_plane[:, e * HALVES + h, :],
+                        rhs=words[:, cols].bitcast(FP8X4),
+                        rhs_scale=scales[:, cols],
+                        start=(h == 0),
+                        stop=(h == HALVES - 1),
+                    )
+            dx = sb("dx%d" % e, [P, C], F32)
+            nc.scalar.copy(dx[:], dx_sums[:])
+            nc.vector.tensor_copy(result[:].indirect(list_of(e * TILES_PER_EXPERT, TILES_PER_EXPERT)), dx[:])
         nc.sync.dma_start(out=out, in_=result[:])

@@ -60,10 +60,6 @@ def tile_moe_bdx_mlp_relu_kernel(
         gate_rows = shared.tile([P, P], F32, name="gate_rows", tag="gate_rows_then_last_words", align_bytes=64)
         gate_col = sb("gate_col", [P, TILES], F32)
         ident = sb("ident", [P, P], F32)
-        warm = sb("warm", [P, 16], F32)
-
-        nc.vector.memset(warm[:, 0:1], 0.0)
-        nc.scalar.copy(warm[:, 8:9], warm[:, 0:1])
 
         nc.gpsimd.memset(dy_plane[:].bitcast(I32), 0)
         nc.vector.memset(gate_rows[:], 0.0)
@@ -84,11 +80,10 @@ def tile_moe_bdx_mlp_relu_kernel(
         load_w2(0)
         nc.sync.dma_start(out=gate_rows[0:TILES, :], in_=gate[0].rearrange("(j p) -> j p", p=P))
         load_scale_rows(nc, w2_plane, w2_scales.rearrange("e s f w -> (e s) f w"))
-        load_a(0, 0)
         load_w2(1)
-        load_a(0, 1)
-        load_a(1, 0)
-        load_a(1, 1)
+        for e in range(E):
+            for h in range(HALVES):
+                load_a(e, h)
         load_scale_rows(nc, w1_plane, w1_scales.rearrange("e s f w -> (e s) f w"))
         nc.sync.dma_start(out=w1_sb[:].bitcast(I32), in_=w1_words.bitcast(I32).rearrange("e s p w -> p (e s) w"))
 
@@ -139,7 +134,7 @@ def tile_moe_bdx_mlp_relu_kernel(
             )
             return gated
 
-        def quantised_da(e, h):
+        def turned_and_mask(e, h):
             gated = [first_product(e, h, jj) for jj in range(TILES_PER_EXPERT)]
             turned = psum.tile([P, 2, C], F32, name="turn_bank", bufs=TURN_BANKS)
             for jj in range(TILES_PER_EXPERT):
@@ -155,19 +150,29 @@ def tile_moe_bdx_mlp_relu_kernel(
                 None,
                 op0=ALU.is_gt,
             )
-            da = sb("da%d%d" % (e, h), [P, C * PACK], BF16)
+            return turned, mask
+
+        def apply_mask(e, h, turned, mask):
+            da = sb("a_sb01" if (e, h) == (0, 0) else "da%d%d" % (e, h), [P, C * PACK], BF16)
             nc.vector.tensor_tensor(
                 da[:].rearrange("p (c u v) -> p c u v", u=2, v=2),
                 turned[:].bitcast(BF16).rearrange("p u (c v) -> p c u v", v=2),
                 mask[:].rearrange("p c (u v) -> p c u v", v=2),
                 ALU.mult,
             )
+            return da
+
+        def quantise(e, h, da):
             words = sb("da_words%d%d" % (e, h), [P, C], U32)
             scales = sb("da_scales%d%d" % (e, h), [P, C], U8)
             nc.vector.quantize_mx(out=words[:].bitcast(FP8X4), scales=scales[:], in_=da[:])
             return words, scales
 
-        da_mx = [[quantised_da(e, h) for h in range(HALVES)] for e in range(E)]
+        da_mx = []
+        for e in range(E):
+            parts = [turned_and_mask(e, h) for h in range(HALVES)]
+            das = [apply_mask(e, h, *parts[h]) for h in range(HALVES)]
+            da_mx.append([quantise(e, h, das[h]) for h in range(HALVES)])
 
         result = sb("result", [P, T], F32)
         for e in range(E):

@@ -61,7 +61,7 @@ def tile_moe_bdx_mlp_relu_kernel(
         gate_col = sb("gate_col", [P, TILES], F32)
         ident = sb("ident", [P, P], F32)
 
-        nc.gpsimd.memset(dy_plane[:].bitcast(I32), 0)
+        nc.vector.memset(dy_plane[:].bitcast(I32), 0)
         nc.vector.memset(gate_rows[:], 0.0)
         nc.vector.memset(w2_plane[:].bitcast(I32), 0)
         make_identity(nc, ident[:])

@@ -27,8 +27,8 @@ TILES_PER_EXPERT = C // P
 TILES = E * TILES_PER_EXPERT
 LIST_ROWS = 16
 RUN = 4
-WORD_GROUPS = ((0,), (1,), (2, 3))
-SUM_BANKS, TURN_BANKS, DX_BANKS = 3, 3, 2
+WORD_GROUPS = ((0, 1), (2, 3))
+SUM_BANKS, TURN_BANKS, DX_BANKS = 4, 2, 2
 
 
 def load_scale_rows(nc, plane, rows):
@@ -44,6 +44,7 @@ def tile_moe_bdx_mlp_relu_kernel(
     with ExitStack() as ctx:
         keep = ctx.enter_context(tc.tile_pool(name="keep", bufs=1))
         shared = ctx.enter_context(tc.tile_pool(name="shared", bufs=1))
+        overlay = ctx.enter_context(tc.tile_pool(name="overlay", bufs=1))
         psum = ctx.enter_context(tc.psum_pool(name="psum", bufs=1))
 
         def sb(name, shape, dtype):
@@ -56,12 +57,13 @@ def tile_moe_bdx_mlp_relu_kernel(
         w2_plane = sb("w2_plane", [P, E * N_PASSES, H], U8)
         w1_sb = sb("w1_sb", [P, E * HALVES, 2 * K], U8)
         w1_plane = sb("w1_plane", [P, E * HALVES, K], U8)
-        a_sb = [[sb("a_sb%d%d" % (e, h), [P, PACK, C], F32) for h in range(HALVES)] for e in range(E)]
+        a_last = overlay.tile([P, PACK, C], F32, name="a_last", align_bytes=64, offset=0)
+        a_sb = [[sb("a_sb00", [P, PACK, C], F32), sb("a_sb01", [P, PACK, C], F32)], [sb("a_sb10", [P, PACK, C], F32), a_last]]
         gate_rows = shared.tile([P, P], F32, name="gate_rows", tag="gate_rows_then_last_words", align_bytes=64)
         gate_col = sb("gate_col", [P, TILES], F32)
         ident = sb("ident", [P, P], F32)
 
-        nc.vector.memset(dy_plane[:].bitcast(I32), 0)
+        nc.gpsimd.memset(dy_plane[:].bitcast(I32), 0)
         nc.vector.memset(gate_rows[:], 0.0)
         nc.vector.memset(w2_plane[:].bitcast(I32), 0)
         make_identity(nc, ident[:])
@@ -134,14 +136,15 @@ def tile_moe_bdx_mlp_relu_kernel(
             )
             return gated
 
-        def turned_and_mask(e, h):
-            gated = [first_product(e, h, jj) for jj in range(TILES_PER_EXPERT)]
+        def turn(gated):
             turned = psum.tile([P, 2, C], F32, name="turn_bank", bufs=TURN_BANKS)
             for jj in range(TILES_PER_EXPERT):
                 pairs = gated[jj][:].bitcast(F32)
                 for u in range(2):
                     nc.tensor.transpose(turned[:, u, jj * P : (jj + 1) * P], pairs[:, u * P : (u + 1) * P], ident[:])
+            return turned
 
+        def make_mask(e, h):
             mask = sb("mask%d%d" % (e, h), [P, C, PACK], BF16)
             nc.vector.tensor_scalar(
                 mask[:].rearrange("p (c r) t -> p c t r", r=RUN),
@@ -150,29 +153,49 @@ def tile_moe_bdx_mlp_relu_kernel(
                 None,
                 op0=ALU.is_gt,
             )
-            return turned, mask
+            return mask
 
-        def apply_mask(e, h, turned, mask):
-            da = sb("a_sb01" if (e, h) == (0, 0) else "da%d%d" % (e, h), [P, C * PACK], BF16)
+        def apply_mask(da, turned, mask):
             nc.vector.tensor_tensor(
-                da[:].rearrange("p (c u v) -> p c u v", u=2, v=2),
+                da.rearrange("p (c u v) -> p c u v", u=2, v=2),
                 turned[:].bitcast(BF16).rearrange("p u (c v) -> p c u v", v=2),
                 mask[:].rearrange("p c (u v) -> p c u v", v=2),
                 ALU.mult,
             )
-            return da
 
-        def quantise(e, h, da):
-            words = sb("da_words%d%d" % (e, h), [P, C], U32)
-            scales = sb("da_scales%d%d" % (e, h), [P, C], U8)
-            nc.vector.quantize_mx(out=words[:].bitcast(FP8X4), scales=scales[:], in_=da[:])
+        def quantise(name, da, columns):
+            words = sb("da_words" + name, [P, columns], U32)
+            scales = sb("da_scales" + name, [P, columns], U8)
+            nc.vector.quantize_mx(out=words[:].bitcast(FP8X4), scales=scales[:], in_=da)
             return words, scales
 
-        da_mx = []
-        for e in range(E):
-            parts = [turned_and_mask(e, h) for h in range(HALVES)]
-            das = [apply_mask(e, h, *parts[h]) for h in range(HALVES)]
-            da_mx.append([quantise(e, h, das[h]) for h in range(HALVES)])
+        units = [(e, h) for e in range(E) for h in range(HALVES)]
+        gated, turned = [], []
+
+        def products(u):
+            gated.append([first_product(*units[u], jj) for jj in range(TILES_PER_EXPERT)])
+
+        relu = [make_mask(*unit) for unit in units]
+        products(0)
+        products(1)
+        turned.append(turn(gated[0]))
+        products(2)
+        turned.append(turn(gated[1]))
+        products(3)
+        first = []
+        for h in range(HALVES):
+            if h == 0:
+                da = sb("a_sb01", [P, C * PACK], BF16)
+            else:
+                da = overlay.tile([P, C * PACK], BF16, name="da01", align_bytes=64, offset=0)
+            apply_mask(da[:], turned[h], relu[h])
+            first.append(da)
+        da_mx = [[quantise("0%d" % h, first[h][:], C) for h in range(HALVES)]]
+        last = overlay.tile([P, HALVES * C * PACK], BF16, name="da1", align_bytes=64, offset=2 * C * PACK)
+        for h in range(HALVES):
+            apply_mask(last[:, h * C * PACK : (h + 1) * C * PACK], turn(gated[HALVES + h]), relu[HALVES + h])
+        words, scales = quantise("1", last[:], HALVES * C)
+        da_mx.append([(words[:, h * C : (h + 1) * C], scales[:, h * C : (h + 1) * C]) for h in range(HALVES)])
 
         result = sb("result", [P, T], F32)
         for e in range(E):

@@ -28,7 +28,8 @@ TILES = E * TILES_PER_EXPERT
 LIST_ROWS = 16
 RUN = 4
 WORD_GROUPS = ((0, 1), (2, 3))
-SUM_BANKS, TURN_BANKS, DX_BANKS = 4, 2, 2
+WARM_PASSES = 3
+SUM_BANKS, TURN_BANKS, DX_BANKS = 4, 3, 1
 
 
 def load_scale_rows(nc, plane, rows):
@@ -53,12 +54,15 @@ def tile_moe_bdx_mlp_relu_kernel(
         offsets = sb("offsets", [P, E * C // LIST_ROWS], U16)
         dy_window = sb("dy_window", [P, N_PASSES, T], I32)
         dy_plane = sb("dy_plane", [P, N_PASSES, T], U8)
-        w2_sb = [sb("w2_sb%d" % e, [P, N_PASSES, 2 * H], U8) for e in range(E)]
+        w2_first = sb("w2_first", [P, N_PASSES, 2 * H], U8)
+        w2_last = [sb("w2_last%d" % o, [P, 2 * H], U8) for o in range(N_PASSES)]
+        w2_sb = [[w2_first[:, o, :] for o in range(N_PASSES)], [t[:] for t in w2_last]]
         w2_plane = sb("w2_plane", [P, E * N_PASSES, H], U8)
         w1_sb = sb("w1_sb", [P, E * HALVES, 2 * K], U8)
         w1_plane = sb("w1_plane", [P, E * HALVES, K], U8)
         a_last = overlay.tile([P, PACK, C], F32, name="a_last", align_bytes=64, offset=0)
-        a_sb = [[sb("a_sb00", [P, PACK, C], F32), sb("a_sb01", [P, PACK, C], F32)], [sb("a_sb10", [P, PACK, C], F32), a_last]]
+        a_first = sb("a_first", [P, PACK, E * C], F32)
+        a_sb = [[a_first[:, :, 0:C], sb("a_sb01", [P, PACK, C], F32)[:]], [a_first[:, :, C : E * C], a_last[:]]]
         gate_rows = shared.tile([P, P], F32, name="gate_rows", tag="gate_rows_then_last_words", align_bytes=64)
         gate_col = sb("gate_col", [P, TILES], F32)
         ident = sb("ident", [P, P], F32)
@@ -66,32 +70,49 @@ def tile_moe_bdx_mlp_relu_kernel(
         nc.gpsimd.memset(dy_plane[:].bitcast(I32), 0)
         nc.vector.memset(gate_rows[:], 0.0)
         nc.vector.memset(w2_plane[:].bitcast(I32), 0)
-        make_identity(nc, ident[:])
         nc.gpsimd.memset(w1_plane[:].bitcast(I32), 0)
-
-        def load_w2(e):
-            nc.sync.dma_start(out=w2_sb[e][:].bitcast(I32), in_=w2_words[e].bitcast(I32).rearrange("s p w -> p s w"))
+        make_identity(nc, ident[:])
 
         def load_a(e, h):
             rows = a[h * PASS : (h + 1) * PASS, e * C : (e + 1) * C]
-            nc.sync.dma_start(out=a_sb[e][h][:], in_=rows.rearrange("(p t) c -> p t c", t=PACK))
+            nc.sync.dma_start(out=a_sb[e][h], in_=rows.rearrange("(p t) c -> p t c", t=PACK))
 
         nc.sync.dma_start(offsets[:], offs)
         nc.sync.dma_start(out=dy_window[:], in_=dy_words.rearrange("o p t d -> p o (t d)").bitcast(I32))
         load_scale_rows(nc, dy_plane, dy_scales)
-        load_w2(0)
         nc.sync.dma_start(out=gate_rows[0:TILES, :], in_=gate[0].rearrange("(j p) -> j p", p=P))
+        nc.sync.dma_start(out=w2_first[:].bitcast(I32), in_=w2_words[0].bitcast(I32).rearrange("s p w -> p s w"))
+        nc.sync.dma_start(out=w2_last[0][:].bitcast(I32), in_=w2_words[1, 0].bitcast(I32))
         load_scale_rows(nc, w2_plane, w2_scales.rearrange("e s f w -> (e s) f w"))
-        load_w2(1)
+        nc.sync.dma_start(out=w2_last[1][:].bitcast(I32), in_=w2_words[1, 1].bitcast(I32))
+        nc.sync.dma_start(out=a_first[:], in_=a[0:PASS, :].rearrange("(p t) c -> p t c", t=PACK))
         for e in range(E):
-            for h in range(HALVES):
-                load_a(e, h)
-        load_scale_rows(nc, w1_plane, w1_scales.rearrange("e s f w -> (e s) f w"))
-        nc.sync.dma_start(out=w1_sb[:].bitcast(I32), in_=w1_words.bitcast(I32).rearrange("e s p w -> p (e s) w"))
+            load_a(e, 1)
 
         gate_turned = psum.tile([P, C], F32, name="dx_bank", bufs=DX_BANKS)
         nc.tensor.transpose(gate_turned[:, 0:P], gate_rows[:], ident[:])
         nc.scalar.copy(gate_col[:], gate_turned[:, 0:TILES])
+
+        warm_in = sb("warm_in", [P, PACK * P], BF16)
+        warm_words = sb("warm_words", [P, P], U32)
+        warm_scales = sb("warm_scales", [P, P], U8)
+        nc.vector.memset(warm_in[:].bitcast(I32), 0)
+        nc.vector.quantize_mx(out=warm_words[:].bitcast(FP8X4), scales=warm_scales[:], in_=warm_in[:])
+        warm_sums = psum.tile([P, PASS], F32, name="dx_bank", bufs=DX_BANKS)
+        for step in range(WARM_PASSES):
+            nc.tensor.matmul_mx(
+                out=warm_sums[:],
+                lhsT=warm_words[:, 0:P].bitcast(FP8X4),
+                lhsT_scale=warm_scales[:, 0:P],
+                rhs=w2_first[:, 0, 0 : 2 * PASS].bitcast(FP4X4),
+                rhs_scale=w1_plane[:].rearrange("p g w -> p (g w)"),
+                start=True,
+                stop=True,
+            )
+
+        load_scale_rows(nc, w1_plane, w1_scales.rearrange("e s f w -> (e s) f w"))
+
+        nc.sync.dma_start(out=w1_sb[:].bitcast(I32), in_=w1_words.bitcast(I32).rearrange("e s p w -> p (e s) w"))
 
         def list_of(first_tile, tiles):
             return offsets[:, first_tile * P // LIST_ROWS : (first_tile + tiles) * P // LIST_ROWS]
@@ -122,7 +143,7 @@ def tile_moe_bdx_mlp_relu_kernel(
                     out=sums[:],
                     lhsT=g_words[j][:, o, :].bitcast(FP8X4),
                     lhsT_scale=g_scales[e][:, o, jj * P : (jj + 1) * P],
-                    rhs=w2_sb[e][:, o, h * 2 * PASS : (h + 1) * 2 * PASS].bitcast(FP4X4),
+                    rhs=w2_sb[e][o][:, h * 2 * PASS : (h + 1) * 2 * PASS].bitcast(FP4X4),
                     rhs_scale=w2_plane[:, e * N_PASSES + o, h * PASS : (h + 1) * PASS],
                     start=(o == 0),
                     stop=(o == N_PASSES - 1),
@@ -148,7 +169,7 @@ def tile_moe_bdx_mlp_relu_kernel(
             mask = sb("mask%d%d" % (e, h), [P, C, PACK], BF16)
             nc.vector.tensor_scalar(
                 mask[:].rearrange("p (c r) t -> p c t r", r=RUN),
-                a_sb[e][h][:].rearrange("p t (c r) -> p c t r", r=RUN),
+                a_sb[e][h].rearrange("p t (c r) -> p c t r", r=RUN),
                 0.0,
                 None,
                 op0=ALU.is_gt,
@@ -182,20 +203,18 @@ def tile_moe_bdx_mlp_relu_kernel(
         products(2)
         turned.append(turn(gated[1]))
         products(3)
-        first = []
-        for h in range(HALVES):
-            if h == 0:
-                da = sb("a_sb01", [P, C * PACK], BF16)
-            else:
-                da = overlay.tile([P, C * PACK], BF16, name="da01", align_bytes=64, offset=0)
-            apply_mask(da[:], turned[h], relu[h])
-            first.append(da)
-        da_mx = [[quantise("0%d" % h, first[h][:], C) for h in range(HALVES)]]
-        last = overlay.tile([P, HALVES * C * PACK], BF16, name="da1", align_bytes=64, offset=2 * C * PACK)
-        for h in range(HALVES):
-            apply_mask(last[:, h * C * PACK : (h + 1) * C * PACK], turn(gated[HALVES + h]), relu[HALVES + h])
-        words, scales = quantise("1", last[:], HALVES * C)
-        da_mx.append([(words[:, h * C : (h + 1) * C], scales[:, h * C : (h + 1) * C]) for h in range(HALVES)])
+        das = [
+            sb("da00", [P, C * PACK], BF16),
+            sb("da01", [P, C * PACK], BF16),
+            overlay.tile([P, C * PACK], BF16, name="da10", align_bytes=64, offset=2 * C * PACK),
+            sb("da11", [P, C * PACK], BF16),
+        ]
+        da_mx = []
+        for e in range(E):
+            mine = range(e * HALVES, (e + 1) * HALVES)
+            for u in mine:
+                apply_mask(das[u][:], turned[u] if u < len(turned) else turn(gated[u]), relu[u])
+            da_mx.append([quantise("%d" % u, das[u][:], C) for u in mine])
 
         result = sb("result", [P, T], F32)
         for e in range(E):

@@ -1,3 +1,4 @@
+import itertools
 from contextlib import ExitStack
 
 import concourse.mybir as mybir
@@ -27,9 +28,10 @@ TILES_PER_EXPERT = C // P
 TILES = E * TILES_PER_EXPERT
 LIST_ROWS = 16
 RUN = 4
-WORD_GROUPS = ((0, 1), (2, 3))
-WARM_PASSES = 3
-SUM_BANKS, TURN_BANKS, DX_BANKS = 4, 3, 1
+LATE_BYTES = 4 * (N_PASSES * E * C - P) + N_PASSES * C
+SUM_BANKS, DX_BANKS = 4, 1
+WARM_WIDTHS = (C, C, PASS, PASS)
+TURN_BANKS = ("turn_bank0", "sum_bank0", "turn_bank1", "turn_bank2")
 
 
 def load_scale_rows(nc, plane, rows):
@@ -44,7 +46,6 @@ def tile_moe_bdx_mlp_relu_kernel(
     nc = tc.nc
     with ExitStack() as ctx:
         keep = ctx.enter_context(tc.tile_pool(name="keep", bufs=1))
-        shared = ctx.enter_context(tc.tile_pool(name="shared", bufs=1))
         overlay = ctx.enter_context(tc.tile_pool(name="overlay", bufs=1))
         psum = ctx.enter_context(tc.psum_pool(name="psum", bufs=1))
 
@@ -52,113 +53,136 @@ def tile_moe_bdx_mlp_relu_kernel(
             return keep.tile(shape, dtype, name=name, align_bytes=64)
 
         offsets = sb("offsets", [P, E * C // LIST_ROWS], U16)
-        dy_window = sb("dy_window", [P, N_PASSES, T], I32)
+        dy_window = [sb("dy_window%d" % o, [P, T], I32) for o in range(N_PASSES)]
         dy_plane = sb("dy_plane", [P, N_PASSES, T], U8)
         w2_first = sb("w2_first", [P, N_PASSES, 2 * H], U8)
-        w2_last = [sb("w2_last%d" % o, [P, 2 * H], U8) for o in range(N_PASSES)]
-        w2_sb = [[w2_first[:, o, :] for o in range(N_PASSES)], [t[:] for t in w2_last]]
-        w2_plane = sb("w2_plane", [P, E * N_PASSES, H], U8)
+        w2_last = [sb("w2_last%d" % h, [P, N_PASSES, 2 * PASS], U8) for h in range(HALVES)]
+        w2_sb = [[w2_first[:, :, h * 2 * PASS : (h + 1) * 2 * PASS] for h in range(HALVES)], [t[:] for t in w2_last]]
+        w2_plane = [sb("w2_plane%d" % e, [P, N_PASSES, H], U8) for e in range(E)]
         w1_sb = sb("w1_sb", [P, E * HALVES, 2 * K], U8)
         w1_plane = sb("w1_plane", [P, E * HALVES, K], U8)
-        a_last = overlay.tile([P, PACK, C], F32, name="a_last", align_bytes=64, offset=0)
-        a_first = sb("a_first", [P, PACK, E * C], F32)
-        a_sb = [[a_first[:, :, 0:C], sb("a_sb01", [P, PACK, C], F32)[:]], [a_first[:, :, C : E * C], a_last[:]]]
-        gate_rows = shared.tile([P, P], F32, name="gate_rows", tag="gate_rows_then_last_words", align_bytes=64)
+        a_sb = [[sb("a_sb%d%d" % (e, h), [P, PACK, C], F32) for h in range(HALVES)] for e in range(E)]
+        gate_room = overlay.tile([P, LATE_BYTES // 4], F32, name="gate_room", align_bytes=64, offset=0)
+        gate_rows = gate_room[:, 0:P]
         gate_col = sb("gate_col", [P, TILES], F32)
         ident = sb("ident", [P, P], F32)
 
         nc.gpsimd.memset(dy_plane[:].bitcast(I32), 0)
-        nc.vector.memset(gate_rows[:], 0.0)
-        nc.vector.memset(w2_plane[:].bitcast(I32), 0)
-        nc.gpsimd.memset(w1_plane[:].bitcast(I32), 0)
+        nc.vector.memset(gate_rows, 0.0)
+        for e in range(E):
+            nc.vector.memset(w2_plane[e][:].bitcast(I32), 0)
         make_identity(nc, ident[:])
+        nc.gpsimd.memset(w1_plane[:].bitcast(I32), 0)
 
         def load_a(e, h):
             rows = a[h * PASS : (h + 1) * PASS, e * C : (e + 1) * C]
-            nc.sync.dma_start(out=a_sb[e][h], in_=rows.rearrange("(p t) c -> p t c", t=PACK))
+            nc.sync.dma_start(out=a_sb[e][h][:], in_=rows.rearrange("(p t) c -> p t c", t=PACK))
+
+        def load_dy(o):
+            nc.sync.dma_start(out=dy_window[o][:], in_=dy_words[o].rearrange("p t d -> p (t d)").bitcast(I32))
+
+        def load_w2(tile, words):
+            nc.sync.dma_start(out=tile[:].bitcast(I32), in_=words.bitcast(I32).rearrange("s p w -> p s w"))
 
         nc.sync.dma_start(offsets[:], offs)
-        nc.sync.dma_start(out=dy_window[:], in_=dy_words.rearrange("o p t d -> p o (t d)").bitcast(I32))
+        load_dy(0)
         load_scale_rows(nc, dy_plane, dy_scales)
         nc.sync.dma_start(out=gate_rows[0:TILES, :], in_=gate[0].rearrange("(j p) -> j p", p=P))
-        nc.sync.dma_start(out=w2_first[:].bitcast(I32), in_=w2_words[0].bitcast(I32).rearrange("s p w -> p s w"))
-        nc.sync.dma_start(out=w2_last[0][:].bitcast(I32), in_=w2_words[1, 0].bitcast(I32))
-        load_scale_rows(nc, w2_plane, w2_scales.rearrange("e s f w -> (e s) f w"))
-        nc.sync.dma_start(out=w2_last[1][:].bitcast(I32), in_=w2_words[1, 1].bitcast(I32))
-        nc.sync.dma_start(out=a_first[:], in_=a[0:PASS, :].rearrange("(p t) c -> p t c", t=PACK))
-        for e in range(E):
-            load_a(e, 1)
+        load_w2(w2_first, w2_words[0])
+        load_dy(1)
+        load_scale_rows(nc, w2_plane[0], w2_scales[0])
+        load_a(0, 0)
+        load_a(0, 1)
+        load_scale_rows(nc, w2_plane[1], w2_scales[1])
+        for h in range(HALVES):
+            load_w2(w2_last[h], w2_words[1, :, :, h * 2 * PASS : (h + 1) * 2 * PASS])
+        load_a(1, 0)
+        load_a(1, 1)
+        load_scale_rows(nc, w1_plane, w1_scales.rearrange("e s f w -> (e s) f w"))
+        nc.sync.dma_start(out=w1_sb[:].bitcast(I32), in_=w1_words.bitcast(I32).rearrange("e s p w -> p (e s) w"))
 
-        gate_turned = psum.tile([P, C], F32, name="dx_bank", bufs=DX_BANKS)
-        nc.tensor.transpose(gate_turned[:, 0:P], gate_rows[:], ident[:])
-        nc.scalar.copy(gate_col[:], gate_turned[:, 0:TILES])
+        def list_of(e):
+            return offsets[:, e * C // LIST_ROWS : (e + 1) * C // LIST_ROWS]
 
-        warm_in = sb("warm_in", [P, PACK * P], BF16)
-        warm_words = sb("warm_words", [P, P], U32)
-        warm_scales = sb("warm_scales", [P, P], U8)
-        nc.vector.memset(warm_in[:].bitcast(I32), 0)
-        nc.vector.quantize_mx(out=warm_words[:].bitcast(FP8X4), scales=warm_scales[:], in_=warm_in[:])
-        warm_sums = psum.tile([P, PASS], F32, name="dx_bank", bufs=DX_BANKS)
-        for step in range(WARM_PASSES):
+        for j in range(TILES):
+            gate_turned = psum.tile([P, P], F32, name="sum_bank%d" % j, bufs=1)
+            nc.tensor.transpose(gate_turned[:], gate_rows, ident[:])
+            nc.scalar.copy(gate_col[:, j : j + 1], gate_turned[:, j : j + 1])
+
+        taken = [0]
+
+        def late(name, columns, dtype, size):
+            tile = overlay.tile([P, columns], dtype, name=name, align_bytes=64, offset=taken[-1])
+            taken.append(taken[-1] + columns * size)
+            return tile[:]
+
+        first_scales = sb("first_scales", [P, N_PASSES * C], U8)
+        g_scales = [
+            [first_scales[:, o * C : (o + 1) * C] for o in range(N_PASSES)],
+            [late("last_scales%d" % o, C, U8, 1) for o in range(N_PASSES)],
+        ]
+        g_words = {}
+
+        def gather_words(words, o, tiles):
+            picks = offsets[:, tiles[0] * P // LIST_ROWS : (tiles[-1] + 1) * P // LIST_ROWS]
+            nc.vector.tensor_copy(words, dy_window[o][:].bitcast(U32).indirect(picks))
+            for place, j in enumerate(tiles):
+                g_words[j, o] = words[:, place * P : (place + 1) * P]
+
+        def gather_scales(e, o):
+            nc.vector.tensor_copy(g_scales[e][o], dy_plane[:, o, :].indirect(list_of(e)))
+
+        gather_words(sb("first_words", [P, P], U32)[:], 0, (0,))
+        gather_scales(0, 0)
+        gather_scales(0, 1)
+        gather_words(late("words00", P, U32, 4), 0, (1,))
+        gather_words(late("words01", C, U32, 4), 1, (0, 1))
+        for o in range(N_PASSES):
+            gather_scales(1, o)
+            gather_words(late("words1%d" % o, C, U32, 4), o, (2, 3))
+
+        for bank, width in enumerate(WARM_WIDTHS):
+            warm_sums = psum.tile([P, width], F32, name="sum_bank%d" % bank, bufs=1)
             nc.tensor.matmul_mx(
                 out=warm_sums[:],
-                lhsT=warm_words[:, 0:P].bitcast(FP8X4),
-                lhsT_scale=warm_scales[:, 0:P],
-                rhs=w2_first[:, 0, 0 : 2 * PASS].bitcast(FP4X4),
-                rhs_scale=w1_plane[:].rearrange("p g w -> p (g w)"),
+                lhsT=g_words[0, 0].bitcast(FP8X4),
+                lhsT_scale=g_scales[0][0][:, 0:P],
+                rhs=w2_first[:, 0, 0 : 2 * width].bitcast(FP4X4),
+                rhs_scale=first_scales[:, 0:width],
                 start=True,
                 stop=True,
             )
 
-        load_scale_rows(nc, w1_plane, w1_scales.rearrange("e s f w -> (e s) f w"))
-
-        nc.sync.dma_start(out=w1_sb[:].bitcast(I32), in_=w1_words.bitcast(I32).rearrange("e s p w -> p (e s) w"))
-
-        def list_of(first_tile, tiles):
-            return offsets[:, first_tile * P // LIST_ROWS : (first_tile + tiles) * P // LIST_ROWS]
-
-        g_words = {}
-        for group in WORD_GROUPS:
-            shape = [P, N_PASSES, P * len(group)]
-            if group == WORD_GROUPS[-1]:
-                words = shared.tile(shape, U32, name="g_words_last", tag="gate_rows_then_last_words", align_bytes=64)
-            else:
-                words = sb("g_words%d" % group[0], shape, U32)
-            for o in range(N_PASSES):
-                window = dy_window[:, o, :].bitcast(U32)
-                nc.vector.tensor_copy(words[:, o, :], window.indirect(list_of(group[0], len(group))))
-            for place, j in enumerate(group):
-                g_words[j] = words[:, :, place * P : (place + 1) * P]
-        g_scales = [sb("g_scales%d" % e, [P, N_PASSES, C], U8) for e in range(E)]
-        for e in range(E):
-            for o in range(N_PASSES):
-                picks = list_of(e * TILES_PER_EXPERT, TILES_PER_EXPERT)
-                nc.vector.tensor_copy(g_scales[e][:, o, :], dy_plane[:, o, :].indirect(picks))
-
-        def first_product(e, h, jj):
-            j = e * TILES_PER_EXPERT + jj
-            sums = psum.tile([P, PASS], F32, name="sum_bank", bufs=SUM_BANKS)
-            for o in range(N_PASSES):
+        def products(e, h):
+            first = (e * HALVES + h) * TILES_PER_EXPERT
+            sums = [
+                psum.tile([P, PASS], F32, name="sum_bank%d" % ((first + jj) % SUM_BANKS), bufs=1)
+                for jj in range(TILES_PER_EXPERT)
+            ]
+            for jj, o in itertools.product(range(TILES_PER_EXPERT), range(N_PASSES)):
                 nc.tensor.matmul_mx(
-                    out=sums[:],
-                    lhsT=g_words[j][:, o, :].bitcast(FP8X4),
-                    lhsT_scale=g_scales[e][:, o, jj * P : (jj + 1) * P],
-                    rhs=w2_sb[e][o][:, h * 2 * PASS : (h + 1) * 2 * PASS].bitcast(FP4X4),
-                    rhs_scale=w2_plane[:, e * N_PASSES + o, h * PASS : (h + 1) * PASS],
+                    out=sums[jj][:],
+                    lhsT=g_words[e * TILES_PER_EXPERT + jj, o].bitcast(FP8X4),
+                    lhsT_scale=g_scales[e][o][:, jj * P : (jj + 1) * P],
+                    rhs=w2_sb[e][h][:, o, :].bitcast(FP4X4),
+                    rhs_scale=w2_plane[e][:, o, h * PASS : (h + 1) * PASS],
                     start=(o == 0),
                     stop=(o == N_PASSES - 1),
                 )
-            gated = sb("gated%d%d" % (j, h), [P, PASS], BF16)
-            nc.scalar.activation(
-                out=gated[:].rearrange("c (u p v) -> c u p v", u=2, v=2),
-                in_=sums[:].rearrange("c (p u v) -> c u p v", u=2, v=2),
-                func=ACT.Copy,
-                scale=gate_col[:, j : j + 1],
-            )
+            gated = []
+            for jj in range(TILES_PER_EXPERT):
+                j = e * TILES_PER_EXPERT + jj
+                gated.append(sb("gated%d%d" % (j, h), [P, PASS], BF16))
+                nc.scalar.activation(
+                    out=gated[jj][:].rearrange("c (u p v) -> c u p v", u=2, v=2),
+                    in_=sums[jj][:].rearrange("c (p u v) -> c u p v", u=2, v=2),
+                    func=ACT.Copy,
+                    scale=gate_col[:, j : j + 1],
+                )
             return gated
 
-        def turn(gated):
-            turned = psum.tile([P, 2, C], F32, name="turn_bank", bufs=TURN_BANKS)
+        def turn(gated, bank):
+            turned = psum.tile([P, 2, C], F32, name=bank, bufs=1)
             for jj in range(TILES_PER_EXPERT):
                 pairs = gated[jj][:].bitcast(F32)
                 for u in range(2):
@@ -169,52 +193,41 @@ def tile_moe_bdx_mlp_relu_kernel(
             mask = sb("mask%d%d" % (e, h), [P, C, PACK], BF16)
             nc.vector.tensor_scalar(
                 mask[:].rearrange("p (c r) t -> p c t r", r=RUN),
-                a_sb[e][h].rearrange("p t (c r) -> p c t r", r=RUN),
+                a_sb[e][h][:].rearrange("p t (c r) -> p c t r", r=RUN),
                 0.0,
                 None,
                 op0=ALU.is_gt,
             )
             return mask
 
-        def apply_mask(da, turned, mask):
+        def apply_mask(e, h, turned, mask):
+            da = sb("da%d%d" % (e, h), [P, C * PACK], BF16)
             nc.vector.tensor_tensor(
-                da.rearrange("p (c u v) -> p c u v", u=2, v=2),
+                da[:].rearrange("p (c u v) -> p c u v", u=2, v=2),
                 turned[:].bitcast(BF16).rearrange("p u (c v) -> p c u v", v=2),
                 mask[:].rearrange("p c (u v) -> p c u v", v=2),
                 ALU.mult,
             )
+            return da
 
-        def quantise(name, da, columns):
-            words = sb("da_words" + name, [P, columns], U32)
-            scales = sb("da_scales" + name, [P, columns], U8)
-            nc.vector.quantize_mx(out=words[:].bitcast(FP8X4), scales=scales[:], in_=da)
+        def quantise(e, h, da):
+            words = sb("da_words%d%d" % (e, h), [P, C], U32)
+            scales = sb("da_scales%d%d" % (e, h), [P, C], U8)
+            nc.vector.quantize_mx(out=words[:].bitcast(FP8X4), scales=scales[:], in_=da[:])
             return words, scales
 
         units = [(e, h) for e in range(E) for h in range(HALVES)]
-        gated, turned = [], []
-
-        def products(u):
-            gated.append([first_product(*units[u], jj) for jj in range(TILES_PER_EXPERT)])
-
         relu = [make_mask(*unit) for unit in units]
-        products(0)
-        products(1)
-        turned.append(turn(gated[0]))
-        products(2)
-        turned.append(turn(gated[1]))
-        products(3)
-        das = [
-            sb("da00", [P, C * PACK], BF16),
-            sb("da01", [P, C * PACK], BF16),
-            overlay.tile([P, C * PACK], BF16, name="da10", align_bytes=64, offset=2 * C * PACK),
-            sb("da11", [P, C * PACK], BF16),
-        ]
-        da_mx = []
-        for e in range(E):
-            mine = range(e * HALVES, (e + 1) * HALVES)
-            for u in mine:
-                apply_mask(das[u][:], turned[u] if u < len(turned) else turn(gated[u]), relu[u])
-            da_mx.append([quantise("%d" % u, das[u][:], C) for u in mine])
+        gated = [products(*units[0])]
+        turned, da_mx = [], []
+        for u in range(len(units)):
+            if u + 1 < len(units):
+                gated.append(products(*units[u + 1]))
+            turned.append(turn(gated[u], TURN_BANKS[u]))
+            if u % HALVES == HALVES - 1:
+                mine = range(u + 1 - HALVES, u + 1)
+                das = [apply_mask(*units[m], turned[m], relu[m]) for m in mine]
+                da_mx.append([quantise(*units[m], da) for m, da in zip(mine, das)])
 
         result = sb("result", [P, T], F32)
         for e in range(E):
@@ -234,5 +247,5 @@ def tile_moe_bdx_mlp_relu_kernel(
                     )
             dx = sb("dx%d" % e, [P, C], F32)
             nc.scalar.copy(dx[:], dx_sums[:])
-            nc.vector.tensor_copy(result[:].indirect(list_of(e * TILES_PER_EXPERT, TILES_PER_EXPERT)), dx[:])
+            nc.vector.tensor_copy(result[:].indirect(list_of(e)), dx[:])
         nc.sync.dma_start(out=out, in_=result[:])

@@ -30,7 +30,6 @@ LIST_ROWS = 16
 RUN = 4
 LATE_BYTES = 4 * (N_PASSES * E * C - P) + N_PASSES * C
 SUM_BANKS, DX_BANKS = 4, 1
-WARM_WIDTHS = (C, C, PASS, PASS)
 TURN_BANKS = ("turn_bank0", "sum_bank0", "turn_bank1", "turn_bank2")
 
 
@@ -140,18 +139,6 @@ def tile_moe_bdx_mlp_relu_kernel(
         for o in range(N_PASSES):
             gather_scales(1, o)
             gather_words(late("words1%d" % o, C, U32, 4), o, (2, 3))
-
-        for bank, width in enumerate(WARM_WIDTHS):
-            warm_sums = psum.tile([P, width], F32, name="sum_bank%d" % bank, bufs=1)
-            nc.tensor.matmul_mx(
-                out=warm_sums[:],
-                lhsT=g_words[0, 0].bitcast(FP8X4),
-                lhsT_scale=g_scales[0][0][:, 0:P],
-                rhs=w2_first[:, 0, 0 : 2 * width].bitcast(FP4X4),
-                rhs_scale=first_scales[:, 0:width],
-                start=True,
-                stop=True,
-            )
 
         def products(e, h):
             first = (e * HALVES + h) * TILES_PER_EXPERT

@@ -1,4 +1,3 @@
-import itertools
 from contextlib import ExitStack
 
 import concourse.mybir as mybir
@@ -29,14 +28,13 @@ TILES = E * TILES_PER_EXPERT
 LIST_ROWS = 16
 RUN = 4
 LATE_BYTES = 4 * (N_PASSES * E * C - P) + N_PASSES * C
-SUM_BANKS, DX_BANKS = 4, 1
-TURN_BANKS = ("turn_bank0", "sum_bank0", "turn_bank1", "turn_bank2")
+SUM_BANKS, TURN_BANKS = 4, 3
 
 
-def load_scale_rows(nc, plane, rows):
+def load_scale_rows(queue, plane, rows):
     by_row = rows.bitcast(I32).rearrange("g (q r) w -> r q g w", r=4)
     for r in range(4):
-        nc.sync.dma_start(out=plane[r:P:32, :, :].bitcast(I32), in_=by_row[r])
+        queue.dma_start(out=plane[r:P:32, :, :].bitcast(I32), in_=by_row[r])
 
 
 def tile_moe_bdx_mlp_relu_kernel(
@@ -60,7 +58,9 @@ def tile_moe_bdx_mlp_relu_kernel(
         w2_plane = [sb("w2_plane%d" % e, [P, N_PASSES, H], U8) for e in range(E)]
         w1_sb = sb("w1_sb", [P, E * HALVES, 2 * K], U8)
         w1_plane = sb("w1_plane", [P, E * HALVES, K], U8)
-        a_sb = [[sb("a_sb%d%d" % (e, h), [P, PACK, C], F32) for h in range(HALVES)] for e in range(E)]
+        a_sb = [[sb("a_sb%d%d" % (e, h), [P, PACK, C], F32) for h in range(HALVES)] for e in range(E - 1)]
+        a_last = overlay.tile([P, PACK, C], F32, name="a_last", align_bytes=64, offset=LATE_BYTES)
+        a_sb.append([sb("a_sb10", [P, PACK, C], F32), a_last])
         gate_room = overlay.tile([P, LATE_BYTES // 4], F32, name="gate_room", align_bytes=64, offset=0)
         gate_rows = gate_room[:, 0:P]
         gate_col = sb("gate_col", [P, TILES], F32)
@@ -85,28 +85,27 @@ def tile_moe_bdx_mlp_relu_kernel(
 
         nc.sync.dma_start(offsets[:], offs)
         load_dy(0)
-        load_scale_rows(nc, dy_plane, dy_scales)
+        load_scale_rows(nc.sync, dy_plane, dy_scales)
         nc.sync.dma_start(out=gate_rows[0:TILES, :], in_=gate[0].rearrange("(j p) -> j p", p=P))
         load_w2(w2_first, w2_words[0])
         load_dy(1)
-        load_scale_rows(nc, w2_plane[0], w2_scales[0])
+        load_scale_rows(nc.sync, w2_plane[0], w2_scales[0])
         load_a(0, 0)
         load_a(0, 1)
-        load_scale_rows(nc, w2_plane[1], w2_scales[1])
+        load_scale_rows(nc.sync, w2_plane[1], w2_scales[1])
         for h in range(HALVES):
             load_w2(w2_last[h], w2_words[1, :, :, h * 2 * PASS : (h + 1) * 2 * PASS])
+        nc.sync.dma_start(out=w1_sb[:].bitcast(I32), in_=w1_words.bitcast(I32).rearrange("e s p w -> p (e s) w"))
         load_a(1, 0)
         load_a(1, 1)
-        load_scale_rows(nc, w1_plane, w1_scales.rearrange("e s f w -> (e s) f w"))
-        nc.sync.dma_start(out=w1_sb[:].bitcast(I32), in_=w1_words.bitcast(I32).rearrange("e s p w -> p (e s) w"))
+        load_scale_rows(nc.gpsimd, w1_plane, w1_scales.rearrange("e s f w -> (e s) f w"))
 
-        def list_of(e):
-            return offsets[:, e * C // LIST_ROWS : (e + 1) * C // LIST_ROWS]
+        def picks(first_tile, tiles):
+            return offsets[:, first_tile * P // LIST_ROWS : (first_tile + tiles) * P // LIST_ROWS]
 
-        for j in range(TILES):
-            gate_turned = psum.tile([P, P], F32, name="sum_bank%d" % j, bufs=1)
-            nc.tensor.transpose(gate_turned[:], gate_rows, ident[:])
-            nc.scalar.copy(gate_col[:, j : j + 1], gate_turned[:, j : j + 1])
+        gate_turned = psum.tile([P, P], F32, name="sum_bank0", bufs=1)
+        nc.tensor.transpose(gate_turned[:], gate_rows, ident[:])
+        nc.scalar.copy(gate_col[:], gate_turned[:, 0:TILES])
 
         taken = [0]
 
@@ -122,64 +121,62 @@ def tile_moe_bdx_mlp_relu_kernel(
         ]
         g_words = {}
 
-        def gather_words(words, o, tiles):
-            picks = offsets[:, tiles[0] * P // LIST_ROWS : (tiles[-1] + 1) * P // LIST_ROWS]
-            nc.vector.tensor_copy(words, dy_window[o][:].bitcast(U32).indirect(picks))
-            for place, j in enumerate(tiles):
-                g_words[j, o] = words[:, place * P : (place + 1) * P]
+        def gather_words(words, o, first_tile, tiles):
+            nc.vector.tensor_copy(words, dy_window[o][:].bitcast(U32).indirect(picks(first_tile, tiles)))
+            for place in range(tiles):
+                g_words[first_tile + place, o] = words[:, place * P : (place + 1) * P]
 
         def gather_scales(e, o):
-            nc.vector.tensor_copy(g_scales[e][o], dy_plane[:, o, :].indirect(list_of(e)))
+            nc.vector.tensor_copy(g_scales[e][o], dy_plane[:, o, :].indirect(picks(e * TILES_PER_EXPERT, TILES_PER_EXPERT)))
 
-        gather_words(sb("first_words", [P, P], U32)[:], 0, (0,))
+        gather_words(sb("first_words", [P, P], U32)[:], 0, 0, 1)
         gather_scales(0, 0)
         gather_scales(0, 1)
-        gather_words(late("words00", P, U32, 4), 0, (1,))
-        gather_words(late("words01", C, U32, 4), 1, (0, 1))
+        gather_words(late("words00", P, U32, 4), 0, 1, 1)
+        gather_words(late("words01", C, U32, 4), 1, 0, 2)
         for o in range(N_PASSES):
             gather_scales(1, o)
-            gather_words(late("words1%d" % o, C, U32, 4), o, (2, 3))
+            gather_words(late("words2%d" % o, C, U32, 4), o, 2, 2)
 
         def products(e, h):
-            first = (e * HALVES + h) * TILES_PER_EXPERT
-            sums = [
-                psum.tile([P, PASS], F32, name="sum_bank%d" % ((first + jj) % SUM_BANKS), bufs=1)
-                for jj in range(TILES_PER_EXPERT)
-            ]
-            for jj, o in itertools.product(range(TILES_PER_EXPERT), range(N_PASSES)):
-                nc.tensor.matmul_mx(
-                    out=sums[jj][:],
-                    lhsT=g_words[e * TILES_PER_EXPERT + jj, o].bitcast(FP8X4),
-                    lhsT_scale=g_scales[e][o][:, jj * P : (jj + 1) * P],
-                    rhs=w2_sb[e][h][:, o, :].bitcast(FP4X4),
-                    rhs_scale=w2_plane[e][:, o, h * PASS : (h + 1) * PASS],
-                    start=(o == 0),
-                    stop=(o == N_PASSES - 1),
-                )
             gated = []
             for jj in range(TILES_PER_EXPERT):
                 j = e * TILES_PER_EXPERT + jj
+                sums = psum.tile([P, PASS], F32, name="sum_bank%d" % ((h * TILES_PER_EXPERT + jj) % SUM_BANKS), bufs=1)
+                for o in range(N_PASSES):
+                    nc.tensor.matmul_mx(
+                        out=sums[:],
+                        lhsT=g_words[j, o].bitcast(FP8X4),
+                        lhsT_scale=g_scales[e][o][:, jj * P : (jj + 1) * P],
+                        rhs=w2_sb[e][h][:, o, :].bitcast(FP4X4),
+                        rhs_scale=w2_plane[e][:, o, h * PASS : (h + 1) * PASS],
+                        start=(o == 0),
+                        stop=(o == N_PASSES - 1),
+                    )
                 gated.append(sb("gated%d%d" % (j, h), [P, PASS], BF16))
                 nc.scalar.activation(
                     out=gated[jj][:].rearrange("c (u p v) -> c u p v", u=2, v=2),
-                    in_=sums[jj][:].rearrange("c (p u v) -> c u p v", u=2, v=2),
+                    in_=sums[:].rearrange("c (p u v) -> c u p v", u=2, v=2),
                     func=ACT.Copy,
                     scale=gate_col[:, j : j + 1],
                 )
             return gated
 
-        def turn(gated, bank):
-            turned = psum.tile([P, 2, C], F32, name=bank, bufs=1)
-            for jj in range(TILES_PER_EXPERT):
-                pairs = gated[jj][:].bitcast(F32)
+        turns = [0]
+
+        def turn(gated):
+            turned = psum.tile([P, 2, len(gated) * P], F32, name="turn_bank%d" % (turns[-1] % TURN_BANKS), bufs=1)
+            turns.append(turns[-1] + 1)
+            for place, tile in enumerate(gated):
+                pairs = tile[:].bitcast(F32)
                 for u in range(2):
-                    nc.tensor.transpose(turned[:, u, jj * P : (jj + 1) * P], pairs[:, u * P : (u + 1) * P], ident[:])
+                    nc.tensor.transpose(turned[:, u, place * P : (place + 1) * P], pairs[:, u * P : (u + 1) * P], ident[:])
             return turned
 
         def make_mask(e, h):
-            mask = sb("mask%d%d" % (e, h), [P, C, PACK], BF16)
+            mask = sb("mask%d%d" % (e, h), [P, C * PACK], BF16)
             nc.vector.tensor_scalar(
-                mask[:].rearrange("p (c r) t -> p c t r", r=RUN),
+                mask[:].rearrange("p (c r t) -> p c t r", r=RUN, t=PACK),
                 a_sb[e][h][:].rearrange("p t (c r) -> p c t r", r=RUN),
                 0.0,
                 None,
@@ -187,52 +184,56 @@ def tile_moe_bdx_mlp_relu_kernel(
             )
             return mask
 
-        def apply_mask(e, h, turned, mask):
-            da = sb("da%d%d" % (e, h), [P, C * PACK], BF16)
+        def apply_mask(da, turned, mask):
             nc.vector.tensor_tensor(
                 da[:].rearrange("p (c u v) -> p c u v", u=2, v=2),
                 turned[:].bitcast(BF16).rearrange("p u (c v) -> p c u v", v=2),
-                mask[:].rearrange("p c (u v) -> p c u v", v=2),
+                mask.rearrange("p (c u v) -> p c u v", u=2, v=2),
                 ALU.mult,
             )
             return da
 
-        def quantise(e, h, da):
-            words = sb("da_words%d%d" % (e, h), [P, C], U32)
-            scales = sb("da_scales%d%d" % (e, h), [P, C], U8)
+        def quantise(name, da):
+            width = da.shape[1] // PACK
+            words = sb("da_words" + name, [P, width], U32)
+            scales = sb("da_scales" + name, [P, width], U8)
             nc.vector.quantize_mx(out=words[:].bitcast(FP8X4), scales=scales[:], in_=da[:])
-            return words, scales
-
-        units = [(e, h) for e in range(E) for h in range(HALVES)]
-        relu = [make_mask(*unit) for unit in units]
-        gated = [products(*units[0])]
-        turned, da_mx = [], []
-        for u in range(len(units)):
-            if u + 1 < len(units):
-                gated.append(products(*units[u + 1]))
-            turned.append(turn(gated[u], TURN_BANKS[u]))
-            if u % HALVES == HALVES - 1:
-                mine = range(u + 1 - HALVES, u + 1)
-                das = [apply_mask(*units[m], turned[m], relu[m]) for m in mine]
-                da_mx.append([quantise(*units[m], da) for m, da in zip(mine, das)])
+            return words[:], scales[:]
 
         result = sb("result", [P, T], F32)
-        for e in range(E):
-            dx_sums = psum.tile([P, C], F32, name="dx_bank", bufs=DX_BANKS)
-            for jj in range(TILES_PER_EXPERT):
-                cols = slice(jj * P, (jj + 1) * P)
-                for h in range(HALVES):
-                    words, scales = da_mx[e][h]
-                    nc.tensor.matmul_mx(
-                        out=dx_sums[:, cols],
-                        lhsT=w1_sb[:, e * HALVES + h, :].bitcast(FP4X4),
-                        lhsT_scale=w1_plane[:, e * HALVES + h, :],
-                        rhs=words[:, cols].bitcast(FP8X4),
-                        rhs_scale=scales[:, cols],
-                        start=(h == 0),
-                        stop=(h == HALVES - 1),
-                    )
-            dx = sb("dx%d" % e, [P, C], F32)
-            nc.scalar.copy(dx[:], dx_sums[:])
-            nc.vector.tensor_copy(result[:].indirect(list_of(e)), dx[:])
+
+        def way_back(e, first_tile, halves, bank, copy):
+            width = halves[0][0].shape[1]
+            dx_sums = psum.tile([P, width], F32, name=bank, bufs=1)
+            for h, (words, scales) in enumerate(halves):
+                nc.tensor.matmul_mx(
+                    out=dx_sums[:],
+                    lhsT=w1_sb[:, e * HALVES + h, :].bitcast(FP4X4),
+                    lhsT_scale=w1_plane[:, e * HALVES + h, :],
+                    rhs=words.bitcast(FP8X4),
+                    rhs_scale=scales,
+                    start=(h == 0),
+                    stop=(h == HALVES - 1),
+                )
+            dx = sb("dx%d" % first_tile, [P, width], F32)
+            copy(dx[:], dx_sums[:])
+            nc.scalar.activation(result[:].indirect(picks(first_tile, width // P)), dx[:], ACT.Copy)
+
+        relu = [make_mask(0, h) for h in range(HALVES)]
+        gated = [products(0, h) for h in range(HALVES)]
+        das = [apply_mask(sb("da0%d" % h, [P, C * PACK], BF16), turn(gated[h]), relu[h][:]) for h in range(HALVES)]
+        first_mx = [quantise("0%d" % h, das[h]) for h in range(HALVES)]
+
+        gated = [products(1, h) for h in range(HALVES)]
+        way_back(0, 0, first_mx, "dx_bank", nc.scalar.copy)
+        relu = [make_mask(1, h) for h in range(HALVES)]
+        low_da = overlay.tile([P, C * PACK], BF16, name="low_da", align_bytes=64, offset=LATE_BYTES)
+        apply_mask(low_da, turn(gated[0]), relu[0][:])
+        turned = [turn([tile]) for tile in gated[1]]
+        low_mx = None
+        for jj, copy in enumerate((nc.scalar.copy, nc.vector.tensor_copy)):
+            da = apply_mask(sb("da11%d" % jj, [P, PASS], BF16), turned[jj], relu[1][:, jj * PASS : (jj + 1) * PASS])
+            low_mx = low_mx or quantise("10", low_da)
+            low = tuple(part[:, jj * P : (jj + 1) * P] for part in low_mx)
+            way_back(1, TILES_PER_EXPERT + jj, [low, quantise("11%d" % jj, da)], "sum_bank%d" % jj, copy)
         nc.sync.dma_start(out=out, in_=result[:])

@@ -27,7 +27,7 @@ TILES_PER_EXPERT = C // P
 TILES = E * TILES_PER_EXPERT
 LIST_ROWS = 16
 RUN = 4
-LATE_BYTES = 4 * (N_PASSES * E * C - P) + N_PASSES * C
+LATE_BYTES = 4 * (N_PASSES * E * C - P) + (N_PASSES * E - 1) * C
 SUM_BANKS, TURN_BANKS = 4, 3
 
 
@@ -103,7 +103,7 @@ def tile_moe_bdx_mlp_relu_kernel(
         def picks(first_tile, tiles):
             return offsets[:, first_tile * P // LIST_ROWS : (first_tile + tiles) * P // LIST_ROWS]
 
-        gate_turned = psum.tile([P, P], F32, name="sum_bank0", bufs=1)
+        gate_turned = psum.tile([P, P], F32, name="dx_bank", bufs=1)
         nc.tensor.transpose(gate_turned[:], gate_rows, ident[:])
         nc.scalar.copy(gate_col[:], gate_turned[:, 0:TILES])
 
@@ -114,9 +114,8 @@ def tile_moe_bdx_mlp_relu_kernel(
             taken.append(taken[-1] + columns * size)
             return tile[:]
 
-        first_scales = sb("first_scales", [P, N_PASSES * C], U8)
         g_scales = [
-            [first_scales[:, o * C : (o + 1) * C] for o in range(N_PASSES)],
+            [sb("first_scales", [P, C], U8)[:], late("second_scales", C, U8, 1)],
             [late("last_scales%d" % o, C, U8, 1) for o in range(N_PASSES)],
         ]
         g_words = {}
@@ -131,12 +130,24 @@ def tile_moe_bdx_mlp_relu_kernel(
 
         gather_words(sb("first_words", [P, P], U32)[:], 0, 0, 1)
         gather_scales(0, 0)
-        gather_scales(0, 1)
         gather_words(late("words00", P, U32, 4), 0, 1, 1)
+        gather_scales(0, 1)
         gather_words(late("words01", C, U32, 4), 1, 0, 2)
         for o in range(N_PASSES):
             gather_scales(1, o)
             gather_words(late("words2%d" % o, C, U32, 4), o, 2, 2)
+
+        warm = psum.tile([P, PASS], F32, name="turn_bank2", bufs=1)
+        for n in range(3):
+            nc.tensor.matmul_mx(
+                out=warm[:, n % 2 * C : (n % 2 + 1) * C],
+                lhsT=g_words[1, 0].bitcast(FP8X4),
+                lhsT_scale=g_scales[0][0][:, P:C],
+                rhs=w2_first[:, 0, 0 : 2 * C].bitcast(FP4X4),
+                rhs_scale=g_scales[0][0],
+                start=True,
+                stop=True,
+            )
 
         def products(e, h):
             gated = []
@@ -153,13 +164,15 @@ def tile_moe_bdx_mlp_relu_kernel(
                         start=(o == 0),
                         stop=(o == N_PASSES - 1),
                     )
-                gated.append(sb("gated%d%d" % (j, h), [P, PASS], BF16))
-                nc.scalar.activation(
-                    out=gated[jj][:].rearrange("c (u p v) -> c u p v", u=2, v=2),
-                    in_=sums[:].rearrange("c (p u v) -> c u p v", u=2, v=2),
-                    func=ACT.Copy,
-                    scale=gate_col[:, j : j + 1],
-                )
+                ordered = sums[:].rearrange("c (p u v) -> c u p v", u=2, v=2)
+                if (j, h) == (TILES - 1, HALVES - 1):
+                    gated.append(overlay.tile([P, PASS], BF16, name="last_gated", align_bytes=64, offset=LATE_BYTES + 2 * C * PACK))
+                    into = gated[jj][:].rearrange("c (u p v) -> c u p v", u=2, v=2)
+                    nc.vector.tensor_scalar(into, ordered, gate_col[:, j : j + 1], None, op0=ALU.mult)
+                else:
+                    gated.append(sb("gated%d%d" % (j, h), [P, PASS], BF16))
+                    into = gated[jj][:].rearrange("c (u p v) -> c u p v", u=2, v=2)
+                    nc.scalar.activation(out=into, in_=ordered, func=ACT.Copy, scale=gate_col[:, j : j + 1])
             return gated
 
         turns = [0]
@@ -224,9 +237,9 @@ def tile_moe_bdx_mlp_relu_kernel(
         das = [apply_mask(sb("da0%d" % h, [P, C * PACK], BF16), turn(gated[h]), relu[h][:]) for h in range(HALVES)]
         first_mx = [quantise("0%d" % h, das[h]) for h in range(HALVES)]
 
+        relu = [make_mask(1, h) for h in range(HALVES)]
         gated = [products(1, h) for h in range(HALVES)]
         way_back(0, 0, first_mx, "dx_bank", nc.scalar.copy)
-        relu = [make_mask(1, h) for h in range(HALVES)]
         low_da = overlay.tile([P, C * PACK], BF16, name="low_da", align_bytes=64, offset=LATE_BYTES)
         apply_mask(low_da, turn(gated[0]), relu[0][:])
         turned = [turn([tile]) for tile in gated[1]]

@@ -52,15 +52,10 @@ def tile_moe_bdx_mlp_relu_kernel(
         offsets = sb("offsets", [P, E * C // LIST_ROWS], U16)
         dy_window = [sb("dy_window%d" % o, [P, T], I32) for o in range(N_PASSES)]
         dy_plane = sb("dy_plane", [P, N_PASSES, T], U8)
-        w2_first = sb("w2_first", [P, N_PASSES, 2 * H], U8)
-        w2_last = [sb("w2_last%d" % h, [P, N_PASSES, 2 * PASS], U8) for h in range(HALVES)]
-        w2_sb = [[w2_first[:, :, h * 2 * PASS : (h + 1) * 2 * PASS] for h in range(HALVES)], [t[:] for t in w2_last]]
+        w2_sb = [[sb("w2_sb%d%d" % (e, h), [P, N_PASSES, 2 * PASS], U8) for h in range(HALVES)] for e in range(E)]
         w2_plane = [sb("w2_plane%d" % e, [P, N_PASSES, H], U8) for e in range(E)]
-        w1_sb = sb("w1_sb", [P, E * HALVES, 2 * K], U8)
+        w1_sb = [sb("w1_sb%d" % e, [P, HALVES, 2 * K], U8) for e in range(E)]
         w1_plane = sb("w1_plane", [P, E * HALVES, K], U8)
-        a_sb = [[sb("a_sb%d%d" % (e, h), [P, PACK, C], F32) for h in range(HALVES)] for e in range(E - 1)]
-        a_last = overlay.tile([P, PACK, C], F32, name="a_last", align_bytes=64, offset=LATE_BYTES)
-        a_sb.append([sb("a_sb10", [P, PACK, C], F32), a_last])
         gate_room = overlay.tile([P, LATE_BYTES // 4], F32, name="gate_room", align_bytes=64, offset=0)
         gate_rows = gate_room[:, 0:P]
         gate_col = sb("gate_col", [P, TILES], F32)
@@ -73,31 +68,41 @@ def tile_moe_bdx_mlp_relu_kernel(
         make_identity(nc, ident[:])
         nc.gpsimd.memset(w1_plane[:].bitcast(I32), 0)
 
-        def load_a(e, h):
-            rows = a[h * PASS : (h + 1) * PASS, e * C : (e + 1) * C]
-            nc.sync.dma_start(out=a_sb[e][h][:], in_=rows.rearrange("(p t) c -> p t c", t=PACK))
+        a_sb = {}
+
+        def load_a(h, first_tile, tiles):
+            a_sb[h, first_tile] = sb("a_sb%d%d" % (h, first_tile), [P, PACK, tiles * P], F32)
+            rows = a[h * PASS : (h + 1) * PASS, first_tile * P : (first_tile + tiles) * P]
+            nc.sync.dma_start(out=a_sb[h, first_tile][:], in_=rows.rearrange("(p t) c -> p t c", t=PACK))
+
+        def load_w1(e):
+            nc.sync.dma_start(out=w1_sb[e][:].bitcast(I32), in_=w1_words[e].bitcast(I32).rearrange("s p w -> p s w"))
 
         def load_dy(o):
             nc.sync.dma_start(out=dy_window[o][:], in_=dy_words[o].rearrange("p t d -> p (t d)").bitcast(I32))
 
-        def load_w2(tile, words):
-            nc.sync.dma_start(out=tile[:].bitcast(I32), in_=words.bitcast(I32).rearrange("s p w -> p s w"))
+        def load_w2(e, h):
+            words = w2_words[e, :, :, h * 2 * PASS : (h + 1) * 2 * PASS]
+            nc.sync.dma_start(out=w2_sb[e][h][:].bitcast(I32), in_=words.bitcast(I32).rearrange("s p w -> p s w"))
 
         nc.sync.dma_start(offsets[:], offs)
         load_dy(0)
         load_scale_rows(nc.sync, dy_plane, dy_scales)
         nc.sync.dma_start(out=gate_rows[0:TILES, :], in_=gate[0].rearrange("(j p) -> j p", p=P))
-        load_w2(w2_first, w2_words[0])
+        load_w2(0, 0)
         load_dy(1)
         load_scale_rows(nc.sync, w2_plane[0], w2_scales[0])
-        load_a(0, 0)
-        load_a(0, 1)
+        load_w2(0, 1)
+        for h in range(HALVES):
+            load_a(h, 0, TILES_PER_EXPERT)
         load_scale_rows(nc.sync, w2_plane[1], w2_scales[1])
         for h in range(HALVES):
-            load_w2(w2_last[h], w2_words[1, :, :, h * 2 * PASS : (h + 1) * 2 * PASS])
-        nc.sync.dma_start(out=w1_sb[:].bitcast(I32), in_=w1_words.bitcast(I32).rearrange("e s p w -> p (e s) w"))
-        load_a(1, 0)
-        load_a(1, 1)
+            load_w2(1, h)
+        load_w1(0)
+        for j in range(TILES_PER_EXPERT, TILES):
+            for h in range(HALVES):
+                load_a(h, j, 1)
+        load_w1(1)
         load_scale_rows(nc.gpsimd, w1_plane, w1_scales.rearrange("e s f w -> (e s) f w"))
 
         def picks(first_tile, tiles):
@@ -137,18 +142,6 @@ def tile_moe_bdx_mlp_relu_kernel(
             gather_scales(1, o)
             gather_words(late("words2%d" % o, C, U32, 4), o, 2, 2)
 
-        warm = psum.tile([P, PASS], F32, name="turn_bank2", bufs=1)
-        for n in range(3):
-            nc.tensor.matmul_mx(
-                out=warm[:, n % 2 * C : (n % 2 + 1) * C],
-                lhsT=g_words[1, 0].bitcast(FP8X4),
-                lhsT_scale=g_scales[0][0][:, P:C],
-                rhs=w2_first[:, 0, 0 : 2 * C].bitcast(FP4X4),
-                rhs_scale=g_scales[0][0],
-                start=True,
-                stop=True,
-            )
-
         def products(e, h):
             gated = []
             for jj in range(TILES_PER_EXPERT):
@@ -164,15 +157,13 @@ def tile_moe_bdx_mlp_relu_kernel(
                         start=(o == 0),
                         stop=(o == N_PASSES - 1),
                     )
-                ordered = sums[:].rearrange("c (p u v) -> c u p v", u=2, v=2)
-                if (j, h) == (TILES - 1, HALVES - 1):
-                    gated.append(overlay.tile([P, PASS], BF16, name="last_gated", align_bytes=64, offset=LATE_BYTES + 2 * C * PACK))
-                    into = gated[jj][:].rearrange("c (u p v) -> c u p v", u=2, v=2)
-                    nc.vector.tensor_scalar(into, ordered, gate_col[:, j : j + 1], None, op0=ALU.mult)
-                else:
-                    gated.append(sb("gated%d%d" % (j, h), [P, PASS], BF16))
-                    into = gated[jj][:].rearrange("c (u p v) -> c u p v", u=2, v=2)
-                    nc.scalar.activation(out=into, in_=ordered, func=ACT.Copy, scale=gate_col[:, j : j + 1])
+                gated.append(sb("gated%d%d" % (j, h), [P, PASS], BF16))
+                nc.scalar.activation(
+                    out=gated[jj][:].rearrange("c (u p v) -> c u p v", u=2, v=2),
+                    in_=sums[:].rearrange("c (p u v) -> c u p v", u=2, v=2),
+                    func=ACT.Copy,
+                    scale=gate_col[:, j : j + 1],
+                )
             return gated
 
         turns = [0]
@@ -186,21 +177,21 @@ def tile_moe_bdx_mlp_relu_kernel(
                     nc.tensor.transpose(turned[:, u, place * P : (place + 1) * P], pairs[:, u * P : (u + 1) * P], ident[:])
             return turned
 
-        def make_mask(e, h):
-            mask = sb("mask%d%d" % (e, h), [P, C * PACK], BF16)
+        def make_mask(mask, h, first_tile):
             nc.vector.tensor_scalar(
-                mask[:].rearrange("p (c r t) -> p c t r", r=RUN, t=PACK),
-                a_sb[e][h][:].rearrange("p t (c r) -> p c t r", r=RUN),
+                mask.rearrange("p (c r t) -> p c t r", r=RUN, t=PACK),
+                a_sb[h, first_tile][:].rearrange("p t (c r) -> p c t r", r=RUN),
                 0.0,
                 None,
                 op0=ALU.is_gt,
             )
             return mask
 
-        def apply_mask(da, turned, mask):
+        def apply_mask(name, turned, mask):
+            da = sb("da" + name, list(mask.shape), BF16)
             nc.vector.tensor_tensor(
                 da[:].rearrange("p (c u v) -> p c u v", u=2, v=2),
-                turned[:].bitcast(BF16).rearrange("p u (c v) -> p c u v", v=2),
+                turned.bitcast(BF16).rearrange("p u (c v) -> p c u v", v=2),
                 mask.rearrange("p (c u v) -> p c u v", u=2, v=2),
                 ALU.mult,
             )
@@ -221,7 +212,7 @@ def tile_moe_bdx_mlp_relu_kernel(
             for h, (words, scales) in enumerate(halves):
                 nc.tensor.matmul_mx(
                     out=dx_sums[:],
-                    lhsT=w1_sb[:, e * HALVES + h, :].bitcast(FP4X4),
+                    lhsT=w1_sb[e][:, h, :].bitcast(FP4X4),
                     lhsT_scale=w1_plane[:, e * HALVES + h, :],
                     rhs=words.bitcast(FP8X4),
                     rhs_scale=scales,
@@ -232,21 +223,27 @@ def tile_moe_bdx_mlp_relu_kernel(
             copy(dx[:], dx_sums[:])
             nc.scalar.activation(result[:].indirect(picks(first_tile, width // P)), dx[:], ACT.Copy)
 
-        relu = [make_mask(0, h) for h in range(HALVES)]
         gated = [products(0, h) for h in range(HALVES)]
-        das = [apply_mask(sb("da0%d" % h, [P, C * PACK], BF16), turn(gated[h]), relu[h][:]) for h in range(HALVES)]
+        relu = [make_mask(sb("mask0%d" % h, [P, C * PACK], BF16)[:], h, 0) for h in range(HALVES)]
+        das = [apply_mask("0%d" % h, turn(gated[h])[:], relu[h]) for h in range(HALVES)]
         first_mx = [quantise("0%d" % h, das[h]) for h in range(HALVES)]
 
-        relu = [make_mask(1, h) for h in range(HALVES)]
         gated = [products(1, h) for h in range(HALVES)]
+        turned = [turn([gated[h][0] for h in range(HALVES)])]
         way_back(0, 0, first_mx, "dx_bank", nc.scalar.copy)
-        low_da = overlay.tile([P, C * PACK], BF16, name="low_da", align_bytes=64, offset=LATE_BYTES)
-        apply_mask(low_da, turn(gated[0]), relu[0][:])
-        turned = [turn([tile]) for tile in gated[1]]
-        low_mx = None
-        for jj, copy in enumerate((nc.scalar.copy, nc.vector.tensor_copy)):
-            da = apply_mask(sb("da11%d" % jj, [P, PASS], BF16), turned[jj], relu[1][:, jj * PASS : (jj + 1) * PASS])
-            low_mx = low_mx or quantise("10", low_da)
-            low = tuple(part[:, jj * P : (jj + 1) * P] for part in low_mx)
-            way_back(1, TILES_PER_EXPERT + jj, [low, quantise("11%d" % jj, da)], "sum_bank%d" % jj, copy)
+        turned.append(turn([gated[h][1] for h in range(HALVES)]))
+        third, last = TILES - 2, TILES - 1
+        mask = sb("third_mask", [P, HALVES * PASS], BF16)
+        for h in range(HALVES):
+            make_mask(mask[:, h * PASS : (h + 1) * PASS], h, third)
+        third_da = apply_mask("2", turned[0][:], mask[:])
+        low_mask = make_mask(sb("low_mask", [P, PASS], BF16)[:], 0, last)
+        words, scales = quantise("2", third_da)
+        halves = [(words[:, h * P : (h + 1) * P], scales[:, h * P : (h + 1) * P]) for h in range(HALVES)]
+        way_back(1, third, halves, "sum_bank0", nc.scalar.copy)
+        low_da = apply_mask("30", turned[1][:, :, 0:P], low_mask)
+        high_mask = make_mask(sb("high_mask", [P, PASS], BF16)[:], 1, last)
+        low_mx = quantise("30", low_da)
+        high_mx = quantise("31", apply_mask("31", turned[1][:, :, P : 2 * P], high_mask))
+        way_back(1, last, [low_mx, high_mx], "sum_bank1", nc.vector.tensor_copy)
         nc.sync.dma_start(out=out, in_=result[:])

@@ -28,7 +28,7 @@ TILES = E * TILES_PER_EXPERT
 LIST_ROWS = 16
 RUN = 4
 LATE_BYTES = 4 * (N_PASSES * E * C - P) + (N_PASSES * E - 1) * C
-SUM_BANKS, TURN_BANKS = 4, 3
+SUM_BANKS = 4
 
 
 def load_scale_rows(queue, plane, rows):
@@ -166,11 +166,8 @@ def tile_moe_bdx_mlp_relu_kernel(
                 )
             return gated
 
-        turns = [0]
-
-        def turn(gated):
-            turned = psum.tile([P, 2, len(gated) * P], F32, name="turn_bank%d" % (turns[-1] % TURN_BANKS), bufs=1)
-            turns.append(turns[-1] + 1)
+        def turn(gated, bank):
+            turned = psum.tile([P, 2, len(gated) * P], F32, name=bank, bufs=1)
             for place, tile in enumerate(gated):
                 pairs = tile[:].bitcast(F32)
                 for u in range(2):
@@ -225,25 +222,23 @@ def tile_moe_bdx_mlp_relu_kernel(
 
         gated = [products(0, h) for h in range(HALVES)]
         relu = [make_mask(sb("mask0%d" % h, [P, C * PACK], BF16)[:], h, 0) for h in range(HALVES)]
-        das = [apply_mask("0%d" % h, turn(gated[h])[:], relu[h]) for h in range(HALVES)]
+        das = [apply_mask("0%d" % h, turn(gated[h], "turn_bank%d" % h)[:], relu[h]) for h in range(HALVES)]
         first_mx = [quantise("0%d" % h, das[h]) for h in range(HALVES)]
 
         gated = [products(1, h) for h in range(HALVES)]
-        turned = [turn([gated[h][0] for h in range(HALVES)])]
-        way_back(0, 0, first_mx, "dx_bank", nc.scalar.copy)
-        turned.append(turn([gated[h][1] for h in range(HALVES)]))
+        halves = range(HALVES)
+
+        def tile_masks(j):
+            return [make_mask(sb("mask%d%d" % (j, h), [P, PASS], BF16)[:], h, j) for h in halves]
+
+        def finish(j, relu, banks, dx_bank, copy):
+            turned = [turn([gated[h][j % TILES_PER_EXPERT]], banks[h]) for h in halves]
+            das = [apply_mask("%d%d" % (j, h), turned[h][:], relu[h]) for h in halves]
+            way_back(1, j, [quantise("%d%d" % (j, h), das[h]) for h in halves], dx_bank, copy)
+
         third, last = TILES - 2, TILES - 1
-        mask = sb("third_mask", [P, HALVES * PASS], BF16)
-        for h in range(HALVES):
-            make_mask(mask[:, h * PASS : (h + 1) * PASS], h, third)
-        third_da = apply_mask("2", turned[0][:], mask[:])
-        low_mask = make_mask(sb("low_mask", [P, PASS], BF16)[:], 0, last)
-        words, scales = quantise("2", third_da)
-        halves = [(words[:, h * P : (h + 1) * P], scales[:, h * P : (h + 1) * P]) for h in range(HALVES)]
-        way_back(1, third, halves, "sum_bank0", nc.scalar.copy)
-        low_da = apply_mask("30", turned[1][:, :, 0:P], low_mask)
-        high_mask = make_mask(sb("high_mask", [P, PASS], BF16)[:], 1, last)
-        low_mx = quantise("30", low_da)
-        high_mx = quantise("31", apply_mask("31", turned[1][:, :, P : 2 * P], high_mask))
-        way_back(1, last, [low_mx, high_mx], "sum_bank1", nc.vector.tensor_copy)
+        relu = tile_masks(third)
+        way_back(0, 0, first_mx, "dx_bank", nc.vector.tensor_copy)
+        finish(third, relu, ("turn_bank0", "turn_bank1"), "sum_bank1", nc.scalar.copy)
+        finish(last, tile_masks(last), ("turn_bank2", "sum_bank0"), "sum_bank2", nc.vector.tensor_copy)
         nc.sync.dma_start(out=out, in_=result[:])

@@ -99,9 +99,9 @@ def tile_moe_bdx_mlp_relu_kernel(
         for h in range(HALVES):
             load_w2(1, h)
         load_w1(0)
+        load_a(0, TILES_PER_EXPERT, TILES_PER_EXPERT)
         for j in range(TILES_PER_EXPERT, TILES):
-            for h in range(HALVES):
-                load_a(h, j, 1)
+            load_a(1, j, 1)
         load_w1(1)
         load_scale_rows(nc.gpsimd, w1_plane, w1_scales.rearrange("e s f w -> (e s) f w"))
 
@@ -226,19 +226,28 @@ def tile_moe_bdx_mlp_relu_kernel(
         first_mx = [quantise("0%d" % h, das[h]) for h in range(HALVES)]
 
         gated = [products(1, h) for h in range(HALVES)]
-        halves = range(HALVES)
-
-        def tile_masks(j):
-            return [make_mask(sb("mask%d%d" % (j, h), [P, PASS], BF16)[:], h, j) for h in halves]
-
-        def finish(j, relu, banks, dx_bank, copy):
-            turned = [turn([gated[h][j % TILES_PER_EXPERT]], banks[h]) for h in halves]
-            das = [apply_mask("%d%d" % (j, h), turned[h][:], relu[h]) for h in halves]
-            way_back(1, j, [quantise("%d%d" % (j, h), das[h]) for h in halves], dx_bank, copy)
-
         third, last = TILES - 2, TILES - 1
-        relu = tile_masks(third)
-        way_back(0, 0, first_mx, "dx_bank", nc.vector.tensor_copy)
-        finish(third, relu, ("turn_bank0", "turn_bank1"), "sum_bank1", nc.scalar.copy)
-        finish(last, tile_masks(last), ("turn_bank2", "sum_bank0"), "sum_bank2", nc.vector.tensor_copy)
+        low_mask = make_mask(sb("low_mask", [P, C * PACK], BF16)[:], 0, third)
+        third_mask = make_mask(sb("third_mask", [P, PASS], BF16)[:], 1, third)
+        way_back(0, 0, first_mx, "dx_bank", nc.scalar.copy)
+        low = [turn([gated[0][0]], "turn_bank0"), turn([gated[0][1]], "turn_bank2")]
+        third_turned = turn([gated[1][0]], "turn_bank1")
+        last_turned = psum.tile([P, P, 2], F32, name="sum_bank0", bufs=1)
+        pairs = gated[1][1][:].bitcast(F32)
+        for u in range(2):
+            nc.tensor.transpose(last_turned[:, :, u], pairs[:, u * P : (u + 1) * P], ident[:])
+
+        das = [apply_mask("20", low[0][:], low_mask[:, 0:PASS]), apply_mask("21", third_turned[:], third_mask)]
+        way_back(1, third, [quantise("2%d" % h, das[h]) for h in range(HALVES)], "sum_bank1", nc.vector.tensor_copy)
+        low_da = apply_mask("30", low[1][:], low_mask[:, PASS : 2 * PASS])
+        last_da = sb("last_da", [P, PASS], BF16)
+        nc.vector.scalar_tensor_tensor(
+            last_da[:].rearrange("p (c t) -> p c t", t=PACK),
+            a_sb[1, last][:].rearrange("p t c -> p c t"),
+            0.0,
+            last_turned[:].rearrange("p c u -> p (c u)").bitcast(BF16).rearrange("p (c t) -> p c t", t=PACK),
+            op0=ALU.is_gt,
+            op1=ALU.mult,
+        )
+        way_back(1, last, [quantise("30", low_da), quantise("31", last_da)], "sum_bank2", nc.vector.tensor_copy)
         nc.sync.dma_start(out=out, in_=result[:])

@@ -28,6 +28,7 @@ TILES = E * TILES_PER_EXPERT
 LIST_ROWS = 16
 RUN = 4
 LATE_BYTES = 4 * (N_PASSES * E * C - P) + (N_PASSES * E - 1) * C
+THIRD_AT = 8192
 SUM_BANKS = 4
 
 
@@ -70,8 +71,8 @@ def tile_moe_bdx_mlp_relu_kernel(
 
         a_sb = {}
 
-        def load_a(h, first_tile, tiles):
-            a_sb[h, first_tile] = sb("a_sb%d%d" % (h, first_tile), [P, PACK, tiles * P], F32)
+        def load_a(h, first_tile, tiles, tile=None):
+            a_sb[h, first_tile] = sb("a_sb%d%d" % (h, first_tile), [P, PACK, tiles * P], F32) if tile is None else tile
             rows = a[h * PASS : (h + 1) * PASS, first_tile * P : (first_tile + tiles) * P]
             nc.sync.dma_start(out=a_sb[h, first_tile][:], in_=rows.rearrange("(p t) c -> p t c", t=PACK))
 
@@ -88,7 +89,7 @@ def tile_moe_bdx_mlp_relu_kernel(
         nc.sync.dma_start(offsets[:], offs)
         load_dy(0)
         load_scale_rows(nc.sync, dy_plane, dy_scales)
-        nc.sync.dma_start(out=gate_rows[0:TILES, :], in_=gate[0].rearrange("(j p) -> j p", p=P))
+        nc.sync.dma_start(out=gate_rows[TILES : 2 * TILES, :], in_=gate[0].rearrange("(j p) -> j p", p=P))
         load_w2(0, 0)
         load_dy(1)
         load_scale_rows(nc.sync, w2_plane[0], w2_scales[0])
@@ -100,8 +101,8 @@ def tile_moe_bdx_mlp_relu_kernel(
             load_w2(1, h)
         load_w1(0)
         load_a(0, TILES_PER_EXPERT, TILES_PER_EXPERT)
-        for j in range(TILES_PER_EXPERT, TILES):
-            load_a(1, j, 1)
+        load_a(1, TILES - 2, 1, overlay.tile([P, PACK, P], F32, name="a_third", align_bytes=64, offset=THIRD_AT))
+        load_a(1, TILES - 1, 1)
         load_w1(1)
         load_scale_rows(nc.gpsimd, w1_plane, w1_scales.rearrange("e s f w -> (e s) f w"))
 
@@ -110,7 +111,7 @@ def tile_moe_bdx_mlp_relu_kernel(
 
         gate_turned = psum.tile([P, P], F32, name="dx_bank", bufs=1)
         nc.tensor.transpose(gate_turned[:], gate_rows, ident[:])
-        nc.scalar.copy(gate_col[:], gate_turned[:, 0:TILES])
+        nc.scalar.copy(gate_col[:], gate_turned[:, TILES : 2 * TILES])
 
         taken = [0]
 
@@ -142,9 +143,9 @@ def tile_moe_bdx_mlp_relu_kernel(
             gather_scales(1, o)
             gather_words(late("words2%d" % o, C, U32, 4), o, 2, 2)
 
-        def products(e, h):
+        def products(e, h, places=range(TILES_PER_EXPERT)):
             gated = []
-            for jj in range(TILES_PER_EXPERT):
+            for jj in places:
                 j = e * TILES_PER_EXPERT + jj
                 sums = psum.tile([P, PASS], F32, name="sum_bank%d" % ((h * TILES_PER_EXPERT + jj) % SUM_BANKS), bufs=1)
                 for o in range(N_PASSES):
@@ -159,7 +160,7 @@ def tile_moe_bdx_mlp_relu_kernel(
                     )
                 gated.append(sb("gated%d%d" % (j, h), [P, PASS], BF16))
                 nc.scalar.activation(
-                    out=gated[jj][:].rearrange("c (u p v) -> c u p v", u=2, v=2),
+                    out=gated[-1][:].rearrange("c (u p v) -> c u p v", u=2, v=2),
                     in_=sums[:].rearrange("c (p u v) -> c u p v", u=2, v=2),
                     func=ACT.Copy,
                     scale=gate_col[:, j : j + 1],
@@ -184,10 +185,11 @@ def tile_moe_bdx_mlp_relu_kernel(
             )
             return mask
 
-        def apply_mask(name, turned, mask):
-            da = sb("da" + name, list(mask.shape), BF16)
+        def apply_mask(name, turned, mask, da=None):
+            if da is None:
+                da = sb("da" + name, list(mask.shape), BF16)[:]
             nc.vector.tensor_tensor(
-                da[:].rearrange("p (c u v) -> p c u v", u=2, v=2),
+                da.rearrange("p (c u v) -> p c u v", u=2, v=2),
                 turned.bitcast(BF16).rearrange("p u (c v) -> p c u v", v=2),
                 mask.rearrange("p (c u v) -> p c u v", u=2, v=2),
                 ALU.mult,
@@ -218,36 +220,50 @@ def tile_moe_bdx_mlp_relu_kernel(
                 )
             dx = sb("dx%d" % first_tile, [P, width], F32)
             copy(dx[:], dx_sums[:])
-            nc.scalar.activation(result[:].indirect(picks(first_tile, width // P)), dx[:], ACT.Copy)
+            return dx
+
+        def scatter(first_tile, dx):
+            nc.scalar.activation(result[:].indirect(picks(first_tile, dx.shape[1] // P)), dx[:], ACT.Copy)
 
         gated = [products(0, h) for h in range(HALVES)]
         relu = [make_mask(sb("mask0%d" % h, [P, C * PACK], BF16)[:], h, 0) for h in range(HALVES)]
         das = [apply_mask("0%d" % h, turn(gated[h], "turn_bank%d" % h)[:], relu[h]) for h in range(HALVES)]
         first_mx = [quantise("0%d" % h, das[h]) for h in range(HALVES)]
 
-        gated = [products(1, h) for h in range(HALVES)]
+        gated = [products(1, 0), products(1, 1, range(0, 1))]
         third, last = TILES - 2, TILES - 1
-        low_mask = make_mask(sb("low_mask", [P, C * PACK], BF16)[:], 0, third)
-        third_mask = make_mask(sb("third_mask", [P, PASS], BF16)[:], 1, third)
-        way_back(0, 0, first_mx, "dx_bank", nc.scalar.copy)
-        low = [turn([gated[0][0]], "turn_bank0"), turn([gated[0][1]], "turn_bank2")]
-        third_turned = turn([gated[1][0]], "turn_bank1")
+        late_relu = sb("late_relu", [P, 3, PASS], BF16)
+        make_mask(late_relu[:, 0:2, :].rearrange("p j w -> p (j w)"), 0, third)
+        make_mask(late_relu[:, 2, :], 1, third)
+        first_dx = way_back(0, 0, first_mx, "dx_bank", nc.scalar.copy)
+        gated[1].extend(products(1, 1, range(1, 2)))
+        scatter(0, first_dx)
+        third_turned = [turn([gated[h][0]], "turn_bank%d" % h) for h in range(HALVES)]
+        low_turned = turn([gated[0][1]], "turn_bank2")
         last_turned = psum.tile([P, P, 2], F32, name="sum_bank0", bufs=1)
         pairs = gated[1][1][:].bitcast(F32)
         for u in range(2):
             nc.tensor.transpose(last_turned[:, :, u], pairs[:, u * P : (u + 1) * P], ident[:])
 
-        das = [apply_mask("20", low[0][:], low_mask[:, 0:PASS]), apply_mask("21", third_turned[:], third_mask)]
-        way_back(1, third, [quantise("2%d" % h, das[h]) for h in range(HALVES)], "sum_bank1", nc.vector.tensor_copy)
-        low_da = apply_mask("30", low[1][:], low_mask[:, PASS : 2 * PASS])
-        last_da = sb("last_da", [P, PASS], BF16)
+        third_da = overlay.tile([P, HALVES * PASS], BF16, name="third_da", align_bytes=64, offset=THIRD_AT - 2 * PASS)
+        last_da = overlay.tile([P, HALVES * PASS], BF16, name="last_da", align_bytes=64, offset=THIRD_AT + 2 * PASS)
+        for h in range(HALVES):
+            apply_mask("", third_turned[h][:], late_relu[:, 2 * h, :], third_da[:, h * PASS : (h + 1) * PASS])
+        apply_mask("", low_turned[:], late_relu[:, 1, :], last_da[:, 0:PASS])
+
+        def by_half(words, scales):
+            return [(words[:, h * P : (h + 1) * P], scales[:, h * P : (h + 1) * P]) for h in range(HALVES)]
+
+        third_mx = by_half(*quantise("2", third_da))
+        scatter(third, way_back(1, third, third_mx, "sum_bank1", nc.scalar.copy))
         nc.vector.scalar_tensor_tensor(
-            last_da[:].rearrange("p (c t) -> p c t", t=PACK),
+            last_da[:, PASS : 2 * PASS].rearrange("p (c t) -> p c t", t=PACK),
             a_sb[1, last][:].rearrange("p t c -> p c t"),
             0.0,
             last_turned[:].rearrange("p c u -> p (c u)").bitcast(BF16).rearrange("p (c t) -> p c t", t=PACK),
             op0=ALU.is_gt,
             op1=ALU.mult,
         )
-        way_back(1, last, [quantise("30", low_da), quantise("31", last_da)], "sum_bank2", nc.vector.tensor_copy)
+        last_mx = [quantise("3%d" % h, last_da[:, h * PASS : (h + 1) * PASS]) for h in range(HALVES)]
+        scatter(last, way_back(1, last, last_mx, "sum_bank2", nc.vector.tensor_copy))
         nc.sync.dma_start(out=out, in_=result[:])

@@ -143,6 +143,18 @@ def tile_moe_bdx_mlp_relu_kernel(
             gather_scales(1, o)
             gather_words(late("words2%d" % o, C, U32, 4), o, 2, 2)
 
+        for bank in range(3):
+            idle = psum.tile([P, C], F32, name="turn_bank%d" % bank, bufs=1)
+            nc.tensor.matmul_mx(
+                out=idle[:],
+                lhsT=g_words[1, 0].bitcast(FP8X4),
+                lhsT_scale=g_scales[0][0][:, P : 2 * P],
+                rhs=w2_sb[0][0][:, 0, 0 : 2 * C].bitcast(FP4X4),
+                rhs_scale=g_scales[0][0],
+                start=True,
+                stop=True,
+            )
+
         def products(e, h, places=range(TILES_PER_EXPERT)):
             gated = []
             for jj in places:

from contextlib import ExitStack

import concourse.mybir as mybir
from concourse.masks import make_identity

K, T, E, C, H, N = 128, 512, 2, 256, 1024, 1024
FLOPS = 2 * E * C * (N * H + H * K)
BYTES = N * T * 33 // 32 + E * (N * H + H * K) * 17 // 32 + 4 * H * E * C + 4 * E * C + 2 * 128 * E * C // 16 + 4 * K * T

F32 = mybir.dt.float32
BF16 = mybir.dt.bfloat16
I32 = mybir.dt.int32
U32 = mybir.dt.uint32
U16 = mybir.dt.uint16
U8 = mybir.dt.uint8
FP8X4 = mybir.dt.float8_e4m3fn_x4
FP4X4 = mybir.dt.float4_e2m1fn_x4
ALU = mybir.AluOpType
ACT = mybir.ActivationFunctionType

P = 128
PACK = 4
PASS = P * PACK
N_PASSES = N // PASS
HALVES = H // PASS
TILES_PER_EXPERT = C // P
TILES = E * TILES_PER_EXPERT
LIST_ROWS = 16
RUN = 4
LATE_BYTES = 4 * (N_PASSES * E * C - P) + (N_PASSES * E - 1) * C
THIRD_AT = 8192
SUM_BANKS = 4


def load_scale_rows(queue, plane, rows):
    by_row = rows.bitcast(I32).rearrange("g (q r) w -> r q g w", r=4)
    for r in range(4):
        queue.dma_start(out=plane[r:P:32, :, :].bitcast(I32), in_=by_row[r])


def tile_moe_bdx_mlp_relu_kernel(
    tc, dy_words, dy_scales, a, w2_words, w2_scales, w1_words, w1_scales, gate, offs, out
):
    nc = tc.nc
    with ExitStack() as ctx:
        keep = ctx.enter_context(tc.tile_pool(name="keep", bufs=1))
        overlay = ctx.enter_context(tc.tile_pool(name="overlay", bufs=1))
        psum = ctx.enter_context(tc.psum_pool(name="psum", bufs=1))

        def sb(name, shape, dtype):
            return keep.tile(shape, dtype, name=name, align_bytes=64)

        offsets = sb("offsets", [P, E * C // LIST_ROWS], U16)
        dy_window = [sb("dy_window%d" % o, [P, T], I32) for o in range(N_PASSES)]
        dy_plane = sb("dy_plane", [P, N_PASSES, T], U8)
        w2_sb = [[sb("w2_sb%d%d" % (e, h), [P, N_PASSES, 2 * PASS], U8) for h in range(HALVES)] for e in range(E)]
        w2_plane = [sb("w2_plane%d" % e, [P, N_PASSES, H], U8) for e in range(E)]
        w1_sb = [sb("w1_sb%d" % e, [P, HALVES, 2 * K], U8) for e in range(E)]
        w1_plane = sb("w1_plane", [P, E * HALVES, K], U8)
        gate_room = overlay.tile([P, LATE_BYTES // 4], F32, name="gate_room", align_bytes=64, offset=0)
        gate_rows = gate_room[:, 0:P]
        gate_col = sb("gate_col", [P, TILES], F32)
        ident = sb("ident", [P, P], F32)

        nc.gpsimd.memset(dy_plane[:].bitcast(I32), 0)
        nc.vector.memset(gate_rows, 0.0)
        for e in range(E):
            nc.vector.memset(w2_plane[e][:].bitcast(I32), 0)
        make_identity(nc, ident[:])
        nc.gpsimd.memset(w1_plane[:].bitcast(I32), 0)

        a_sb = {}

        def load_a(h, first_tile, tiles, tile=None):
            a_sb[h, first_tile] = sb("a_sb%d%d" % (h, first_tile), [P, PACK, tiles * P], F32) if tile is None else tile
            rows = a[h * PASS : (h + 1) * PASS, first_tile * P : (first_tile + tiles) * P]
            nc.sync.dma_start(out=a_sb[h, first_tile][:], in_=rows.rearrange("(p t) c -> p t c", t=PACK))

        def load_w1(e):
            nc.sync.dma_start(out=w1_sb[e][:].bitcast(I32), in_=w1_words[e].bitcast(I32).rearrange("s p w -> p s w"))

        def load_dy(o):
            nc.sync.dma_start(out=dy_window[o][:], in_=dy_words[o].rearrange("p t d -> p (t d)").bitcast(I32))

        def load_w2(e, h):
            words = w2_words[e, :, :, h * 2 * PASS : (h + 1) * 2 * PASS]
            nc.sync.dma_start(out=w2_sb[e][h][:].bitcast(I32), in_=words.bitcast(I32).rearrange("s p w -> p s w"))

        nc.sync.dma_start(offsets[:], offs)
        load_dy(0)
        load_scale_rows(nc.sync, dy_plane, dy_scales)
        nc.sync.dma_start(out=gate_rows[TILES : 2 * TILES, :], in_=gate[0].rearrange("(j p) -> j p", p=P))
        load_w2(0, 0)
        load_dy(1)
        load_scale_rows(nc.sync, w2_plane[0], w2_scales[0])
        load_w2(0, 1)
        for h in range(HALVES):
            load_a(h, 0, TILES_PER_EXPERT)
        load_scale_rows(nc.sync, w2_plane[1], w2_scales[1])
        for h in range(HALVES):
            load_w2(1, h)
        load_w1(0)
        load_a(0, TILES_PER_EXPERT, TILES_PER_EXPERT)
        load_a(1, TILES - 2, 1, overlay.tile([P, PACK, P], F32, name="a_third", align_bytes=64, offset=THIRD_AT))
        load_a(1, TILES - 1, 1)
        load_w1(1)
        load_scale_rows(nc.gpsimd, w1_plane, w1_scales.rearrange("e s f w -> (e s) f w"))

        def picks(first_tile, tiles):
            return offsets[:, first_tile * P // LIST_ROWS : (first_tile + tiles) * P // LIST_ROWS]

        gate_turned = psum.tile([P, P], F32, name="dx_bank", bufs=1)
        nc.tensor.transpose(gate_turned[:], gate_rows, ident[:])
        nc.scalar.copy(gate_col[:], gate_turned[:, TILES : 2 * TILES])

        taken = [0]

        def late(name, columns, dtype, size):
            tile = overlay.tile([P, columns], dtype, name=name, align_bytes=64, offset=taken[-1])
            taken.append(taken[-1] + columns * size)
            return tile[:]

        g_scales = [
            [sb("first_scales", [P, C], U8)[:], late("second_scales", C, U8, 1)],
            [late("last_scales%d" % o, C, U8, 1) for o in range(N_PASSES)],
        ]
        g_words = {}

        def gather_words(words, o, first_tile, tiles):
            nc.vector.tensor_copy(words, dy_window[o][:].bitcast(U32).indirect(picks(first_tile, tiles)))
            for place in range(tiles):
                g_words[first_tile + place, o] = words[:, place * P : (place + 1) * P]

        def gather_scales(e, o):
            nc.vector.tensor_copy(g_scales[e][o], dy_plane[:, o, :].indirect(picks(e * TILES_PER_EXPERT, TILES_PER_EXPERT)))

        gather_words(sb("first_words", [P, P], U32)[:], 0, 0, 1)
        gather_scales(0, 0)
        gather_words(late("words00", P, U32, 4), 0, 1, 1)
        gather_scales(0, 1)
        gather_words(late("words01", C, U32, 4), 1, 0, 2)
        for o in range(N_PASSES):
            gather_scales(1, o)
            gather_words(late("words2%d" % o, C, U32, 4), o, 2, 2)

        for bank in range(3):
            idle = psum.tile([P, C], F32, name="turn_bank%d" % bank, bufs=1)
            nc.tensor.matmul_mx(
                out=idle[:],
                lhsT=g_words[1, 0].bitcast(FP8X4),
                lhsT_scale=g_scales[0][0][:, P : 2 * P],
                rhs=w2_sb[0][0][:, 0, 0 : 2 * C].bitcast(FP4X4),
                rhs_scale=g_scales[0][0],
                start=True,
                stop=True,
            )

        def products(e, h, places=range(TILES_PER_EXPERT)):
            gated = []
            for jj in places:
                j = e * TILES_PER_EXPERT + jj
                sums = psum.tile([P, PASS], F32, name="sum_bank%d" % ((h * TILES_PER_EXPERT + jj) % SUM_BANKS), bufs=1)
                for o in range(N_PASSES):
                    nc.tensor.matmul_mx(
                        out=sums[:],
                        lhsT=g_words[j, o].bitcast(FP8X4),
                        lhsT_scale=g_scales[e][o][:, jj * P : (jj + 1) * P],
                        rhs=w2_sb[e][h][:, o, :].bitcast(FP4X4),
                        rhs_scale=w2_plane[e][:, o, h * PASS : (h + 1) * PASS],
                        start=(o == 0),
                        stop=(o == N_PASSES - 1),
                    )
                gated.append(sb("gated%d%d" % (j, h), [P, PASS], BF16))
                nc.scalar.activation(
                    out=gated[-1][:].rearrange("c (u p v) -> c u p v", u=2, v=2),
                    in_=sums[:].rearrange("c (p u v) -> c u p v", u=2, v=2),
                    func=ACT.Copy,
                    scale=gate_col[:, j : j + 1],
                )
            return gated

        def turn(gated, bank):
            turned = psum.tile([P, 2, len(gated) * P], F32, name=bank, bufs=1)
            for place, tile in enumerate(gated):
                pairs = tile[:].bitcast(F32)
                for u in range(2):
                    nc.tensor.transpose(turned[:, u, place * P : (place + 1) * P], pairs[:, u * P : (u + 1) * P], ident[:])
            return turned

        def make_mask(mask, h, first_tile):
            nc.vector.tensor_scalar(
                mask.rearrange("p (c r t) -> p c t r", r=RUN, t=PACK),
                a_sb[h, first_tile][:].rearrange("p t (c r) -> p c t r", r=RUN),
                0.0,
                None,
                op0=ALU.is_gt,
            )
            return mask

        def apply_mask(name, turned, mask, da=None):
            if da is None:
                da = sb("da" + name, list(mask.shape), BF16)[:]
            nc.vector.tensor_tensor(
                da.rearrange("p (c u v) -> p c u v", u=2, v=2),
                turned.bitcast(BF16).rearrange("p u (c v) -> p c u v", v=2),
                mask.rearrange("p (c u v) -> p c u v", u=2, v=2),
                ALU.mult,
            )
            return da

        def quantise(name, da):
            width = da.shape[1] // PACK
            words = sb("da_words" + name, [P, width], U32)
            scales = sb("da_scales" + name, [P, width], U8)
            nc.vector.quantize_mx(out=words[:].bitcast(FP8X4), scales=scales[:], in_=da[:])
            return words[:], scales[:]

        result = sb("result", [P, T], F32)

        def way_back(e, first_tile, halves, bank, copy):
            width = halves[0][0].shape[1]
            dx_sums = psum.tile([P, width], F32, name=bank, bufs=1)
            for h, (words, scales) in enumerate(halves):
                nc.tensor.matmul_mx(
                    out=dx_sums[:],
                    lhsT=w1_sb[e][:, h, :].bitcast(FP4X4),
                    lhsT_scale=w1_plane[:, e * HALVES + h, :],
                    rhs=words.bitcast(FP8X4),
                    rhs_scale=scales,
                    start=(h == 0),
                    stop=(h == HALVES - 1),
                )
            dx = sb("dx%d" % first_tile, [P, width], F32)
            copy(dx[:], dx_sums[:])
            return dx

        def scatter(first_tile, dx):
            nc.scalar.activation(result[:].indirect(picks(first_tile, dx.shape[1] // P)), dx[:], ACT.Copy)

        gated = [products(0, h) for h in range(HALVES)]
        relu = [make_mask(sb("mask0%d" % h, [P, C * PACK], BF16)[:], h, 0) for h in range(HALVES)]
        das = [apply_mask("0%d" % h, turn(gated[h], "turn_bank%d" % h)[:], relu[h]) for h in range(HALVES)]
        first_mx = [quantise("0%d" % h, das[h]) for h in range(HALVES)]

        gated = [products(1, 0), products(1, 1, range(0, 1))]
        third, last = TILES - 2, TILES - 1
        late_relu = sb("late_relu", [P, 3, PASS], BF16)
        make_mask(late_relu[:, 0:2, :].rearrange("p j w -> p (j w)"), 0, third)
        make_mask(late_relu[:, 2, :], 1, third)
        first_dx = way_back(0, 0, first_mx, "dx_bank", nc.scalar.copy)
        gated[1].extend(products(1, 1, range(1, 2)))
        scatter(0, first_dx)
        third_turned = [turn([gated[h][0]], "turn_bank%d" % h) for h in range(HALVES)]
        low_turned = turn([gated[0][1]], "turn_bank2")
        last_turned = psum.tile([P, P, 2], F32, name="sum_bank0", bufs=1)
        pairs = gated[1][1][:].bitcast(F32)
        for u in range(2):
            nc.tensor.transpose(last_turned[:, :, u], pairs[:, u * P : (u + 1) * P], ident[:])

        third_da = overlay.tile([P, HALVES * PASS], BF16, name="third_da", align_bytes=64, offset=THIRD_AT - 2 * PASS)
        last_da = overlay.tile([P, HALVES * PASS], BF16, name="last_da", align_bytes=64, offset=THIRD_AT + 2 * PASS)
        for h in range(HALVES):
            apply_mask("", third_turned[h][:], late_relu[:, 2 * h, :], third_da[:, h * PASS : (h + 1) * PASS])
        apply_mask("", low_turned[:], late_relu[:, 1, :], last_da[:, 0:PASS])

        def by_half(words, scales):
            return [(words[:, h * P : (h + 1) * P], scales[:, h * P : (h + 1) * P]) for h in range(HALVES)]

        third_mx = by_half(*quantise("2", third_da))
        scatter(third, way_back(1, third, third_mx, "sum_bank1", nc.scalar.copy))
        nc.vector.scalar_tensor_tensor(
            last_da[:, PASS : 2 * PASS].rearrange("p (c t) -> p c t", t=PACK),
            a_sb[1, last][:].rearrange("p t c -> p c t"),
            0.0,
            last_turned[:].rearrange("p c u -> p (c u)").bitcast(BF16).rearrange("p (c t) -> p c t", t=PACK),
            op0=ALU.is_gt,
            op1=ALU.mult,
        )
        last_mx = [quantise("3%d" % h, last_da[:, h * PASS : (h + 1) * PASS]) for h in range(HALVES)]
        scatter(last, way_back(1, last, last_mx, "sum_bank2", nc.vector.tensor_copy))
        nc.sync.dma_start(out=out, in_=result[:])
